import numpy as np
import ml_dtypes


def mxq(x, axis, fmt="e4m3"):
    dtype, down = {"e4m3": (ml_dtypes.float8_e4m3fn, 7), "e5m2": (ml_dtypes.float8_e5m2, 14)}[fmt]
    v = np.moveaxis(np.asarray(x, np.float32).astype(ml_dtypes.bfloat16).astype(np.float64), axis, -1)
    blocks = v.reshape(v.shape[:-1] + (-1, 32))
    amax = np.abs(blocks).max(-1, keepdims=True)
    byte = np.maximum(np.where(amax > 0, np.frexp(amax)[1] - 1 + 127, 0) - down, 1)
    scale = np.exp2(byte - 127.0)
    codes = (blocks / scale).astype(np.float32).astype(dtype).astype(np.float64)
    return np.moveaxis((codes * scale).reshape(v.shape), -1, axis)


WIDE = False


def mx_kscale(k):
    if not WIDE:
        return np.ones(k)
    levels = np.array([10, -10, 5, -5, 0])
    if k % 512:
        return np.exp2(np.random.permutation(np.resize(levels, k // 32))).repeat(32)
    a = np.empty((k // 512, 16))
    for p in range(k // 512):
        a[p, :8] = np.random.permutation(np.resize(levels, 8))
        for g in range(8):
            far = levels[np.abs(levels - a[p, g]) >= 10]
            a[p, g + 8] = far[np.random.randint(len(far))]
    return np.exp2(a.ravel()).repeat(32)


def f64(x):
    return np.asarray(x).astype(np.float64)


def striped(idx):
    return np.tile(idx.reshape(-1, 16).T, (8, 1)).astype(np.uint16)


def unstriped(offs):
    return offs[:16].T.reshape(-1).astype(np.int64)


E2M1 = np.array([0.0, 0.5, 1.0, 1.5, 2.0, 3.0, 4.0, 6.0, -0.0, -0.5, -1.0, -1.5, -2.0, -3.0, -4.0, -6.0])


def pack_weight(w, fmt):
    k, n = w.shape
    w = f64(np.asarray(w, np.float32).astype(ml_dtypes.bfloat16)).reshape(k // 32, 32, n)
    amax = np.abs(w).max(1)
    if fmt == "e4m3":
        byte = np.frexp(amax)[1] - 1 + 127 - 7
    else:
        mant, ex = np.frexp(amax / 6.0)
        byte = np.where(mant > 0.5, ex, ex - 1) + 127
    byte = np.clip(np.where(amax > 0, byte, 1), 1, 254)
    scaled = (w * np.exp2(127.0 - byte)[:, None, :]).reshape(k, n).astype(np.float32)
    by_word = np.ascontiguousarray(scaled.reshape(k // 512, 128, 4, n).transpose(0, 1, 3, 2))
    if fmt == "e4m3":
        words = by_word.astype(ml_dtypes.float8_e4m3fn).view(np.uint8)
    else:
        c = by_word.astype(ml_dtypes.float4_e2m1fn).view(np.uint8) & 0xF
        words = (c[..., 0::2] | (c[..., 1::2] << 4)).reshape(k // 512, 128, 2 * n)
    return np.ascontiguousarray(words), np.ascontiguousarray(byte.astype(np.uint8).reshape(k // 512, 16, n))


def unpack_weight(words, scales, fmt):
    g, _, n = scales.shape
    words = np.ascontiguousarray(words).reshape(g, 128, n, -1)
    if fmt == "e4m3":
        vals = words.view(ml_dtypes.float8_e4m3fn).astype(np.float64)
    else:
        nib = np.empty((g, 128, n, 4), np.uint8)
        nib[..., 0::2] = words & 0xF
        nib[..., 1::2] = words >> 4
        vals = E2M1[nib]
    vals = vals * np.repeat(np.exp2(scales.astype(np.float64) - 127.0), 8, axis=1)[..., None]
    return vals.transpose(0, 1, 3, 2).reshape(g * 512, n)


def gelu(v):
    return 0.5 * v * (1.0 + np.tanh(np.sqrt(2.0 / np.pi) * (v + 0.044715 * v**3)))


K, H, N, T, S = 1536, 512, 768, 2048, 1024


def setup_inputs():
    n = np.random.standard_normal
    s = mx_kscale(K)[:, None]
    u = mx_kscale(H)[:, None]
    tab_words, tab_scales = pack_weight(n((K, T)) * s, "e4m3")
    wb_words, wb_scales = pack_weight(n((K, H)) / np.sqrt(K) / s, "e2m1")
    wo_words, wo_scales = pack_weight(1.5 * n((H, N)) / np.sqrt(H) / u, "e4m3")
    return {
        "tab_words": tab_words, "tab_scales": tab_scales,
        "offs": striped(np.random.permutation(T)[:S]),
        "wa": (n((K, H)) / np.sqrt(K) / s).astype(np.float32),
        "wb_words": wb_words, "wb_scales": wb_scales,
        "gT": (0.6 * n((H, T))).astype(np.float32),
        "gain": (np.exp(0.3 * n(H)) * u[:, 0]).astype(np.float32),
        "wo_words": wo_words, "wo_scales": wo_scales,
    }


def reference(tab_words, tab_scales, offs, wa, wb_words, wb_scales, gT, gain, wo_words, wo_scales):
    v = unpack_weight(tab_words, tab_scales, "e4m3")[:, unstriped(offs)]
    g = f64(gT)[:, unstriped(offs)]
    waq = mxq(f64(wa), 0, "e4m3")
    wb = unpack_weight(wb_words, wb_scales, "e2m1")
    wo = unpack_weight(wo_words, wo_scales, "e4m3")
    a = waq.T @ v
    b = wb.T @ v
    gate = 1.0 / (1.0 + np.exp(-b))
    h = f64(gain)[:, None] * (np.tanh(a) * gate + g)
    hq = mxq(h, 0, "e4m3")
    return wo.T @ hq

@@ -1,0 +1,226 @@
+from contextlib import ExitStack
+
+import concourse.mybir as mybir
+
+K, H, N, T, S = 1536, 512, 768, 2048, 1024
+FLOPS = 2 * S * (2 * K * H + H * N)
+
+F32 = mybir.dt.float32
+BF16 = mybir.dt.bfloat16
+I32 = mybir.dt.int32
+U32 = mybir.dt.uint32
+U16 = mybir.dt.uint16
+U8 = mybir.dt.uint8
+FP8X4 = mybir.dt.float8_e4m3fn_x4
+FP4X4 = mybir.dt.float4_e2m1fn_x4
+ACT = mybir.ActivationFunctionType
+ALU = mybir.AluOpType
+
+P = 128
+PACK = 4
+PASSES = K // (P * PACK)
+HALF = 512
+HALVES = S // HALF
+PIECE = 256
+CHUNKS = N // P
+QUADS = 4
+SHIFT_ROWS = 112
+
+
+def tile_list_gated_neighbor_messages_kernel(
+    tc, tab_words, tab_scales, offs, wa, wb_words, wb_scales, gT, gain, wo_words, wo_scales, out
+):
+    nc = tc.nc
+    with ExitStack() as ctx:
+        lists = ctx.enter_context(tc.tile_pool(name="lists", bufs=1))
+        keep = ctx.enter_context(tc.tile_pool(name="keep", bufs=1))
+        ring2 = ctx.enter_context(tc.tile_pool(name="ring2", bufs=2))
+        big = ctx.enter_context(tc.tile_pool(name="big", bufs=4))
+        ring3 = ctx.enter_context(tc.tile_pool(name="ring3", bufs=3))
+        psum = ctx.enter_context(tc.psum_pool(name="psum", bufs=8))
+
+        offsets = lists.tile([P, S // 16], U16, name="offsets")
+        nc.sync.dma_start(offsets[:], offs)
+
+        def held(name, shape, dtype):
+            return keep.tile(shape, dtype, name=name, align_bytes=64)
+
+        tab, wa_raw, g_tab = {}, {}, {}
+        wb_raw = held("wb_raw", [P, PASSES, H // 2], I32)
+        tab_sc = held("tab_sc", [P, T // 4], I32)
+        wb_sc_raw = held("wb_sc_raw", [P, PASSES, H // 4], I32)
+        wo_sc = held("wo_sc", [P, N // 4], I32)
+        v_sc_low = held("v_sc_low", [P, PASSES - 1, S // 4], I32)
+        gain4 = held("gain4", [P, PACK], F32)
+
+        nc.vector.memset(tab_sc[:], 0)
+        nc.vector.memset(wb_sc_raw[:], 0)
+        nc.vector.memset(wo_sc[:], 0)
+        nc.vector.memset(v_sc_low[:], 0)
+
+        def load_tab(a):
+            tab[a] = big.tile([P, T], I32, name="big", align_bytes=64)
+            nc.sync.dma_start(tab[a][:], tab_words[a].rearrange("p n i -> p (n i)").bitcast(I32))
+
+        def load_wa(a):
+            rows = wa[a * P * PACK : (a + 1) * P * PACK, :]
+            wa_raw[a] = big.tile([P, PACK, H], F32, name="big", align_bytes=64)
+            nc.sync.dma_start(wa_raw[a][:], rows.rearrange("(p j) c -> p j c", j=PACK))
+
+        load_tab(0)
+        nc.sync.dma_start(wb_raw[:], wb_words.rearrange("a p c -> p a c").bitcast(I32))
+        load_tab(1)
+        load_wa(0)
+        load_tab(2)
+        load_wa(1)
+        load_wa(2)
+        g_planes = gT.rearrange("(p t) n -> p t n", t=PACK)
+        for t in range(PACK):
+            g_tab[t] = big.tile([P, T], F32, name="big", align_bytes=64)
+            nc.sync.dma_start(g_tab[t][:], g_planes[:, t, :])
+
+        for q in range(QUADS):
+            nc.gpsimd.dma_start(
+                tab_sc[32 * q : 32 * q + 4 * PASSES, :],
+                tab_scales[:, 4 * q : 4 * q + 4, :].bitcast(I32),
+            )
+        for q in range(QUADS):
+            nc.scalar.dma_start(
+                wb_sc_raw[32 * q : 32 * q + 4, :, :],
+                wb_scales[:, 4 * q : 4 * q + 4, :].rearrange("a r c -> r a c").bitcast(I32),
+            )
+        nc.gpsimd.dma_start(gain4[:], gain.rearrange("(p t) -> p t", t=PACK))
+        for q in range(QUADS):
+            nc.gpsimd.dma_start(
+                wo_sc[32 * q : 32 * q + 4, :], wo_scales[0, 4 * q : 4 * q + 4, :].bitcast(I32)
+            )
+
+        v_codes = [held(f"v_codes{a}", [P, S], U32) for a in range(PASSES)]
+        v_sc = held("v_sc", [P, S], U8)
+        wa_codes = [held(f"wa_codes{a}", [P, H], U32) for a in range(PASSES)]
+        wa_sc = [held(f"wa_sc{a}", [P, H], U8) for a in range(PASSES)]
+        wb_codes = held("wb_codes", [P, PASSES, H // 2], I32)
+        wb_sc = held("wb_sc", [P, PASSES, H], U8)
+        gain_wide = held("gain_wide", [P, PACK, HALF], F32)
+
+        def gather_words(a):
+            nc.vector.tensor_copy(v_codes[a][:], tab[a][:].bitcast(U32).indirect(offsets[:]))
+
+        def quantize_wa(a):
+            grouped = ring2.tile([P, H * PACK], BF16, name="wa_grouped", align_bytes=64)
+            nc.scalar.copy(
+                grouped[:].rearrange("p (t m j) -> p m j t", t=PACK, j=PACK),
+                wa_raw[a][:].rearrange("p j (m t) -> p m j t", t=PACK),
+            )
+            nc.vector.quantize_mx(out=wa_codes[a][:].bitcast(FP8X4), scales=wa_sc[a][:], in_=grouped[:])
+
+        gather_words(0)
+        nc.vector.tensor_copy(v_sc[:], tab_sc[:].bitcast(U8).indirect(offsets[:]))
+        for a in range(1, PASSES):
+            nc.scalar.dma_start(
+                v_sc_low[0:SHIFT_ROWS, a - 1, :], v_sc[4 * a : 4 * a + SHIFT_ROWS, :].bitcast(I32)
+            )
+        nc.vector.tensor_copy(
+            wb_codes[:].bitcast(U16).rearrange("p a (t m) -> p a m t", t=PACK),
+            wb_raw[:].bitcast(U16).rearrange("p a (m t) -> p a m t", t=PACK),
+        )
+        nc.vector.tensor_copy(
+            wb_sc[:].rearrange("p a (t m) -> p a m t", t=PACK),
+            wb_sc_raw[:].bitcast(U8).rearrange("p a (m t) -> p a m t", t=PACK),
+        )
+        gather_words(1)
+        quantize_wa(0)
+        gather_words(2)
+        quantize_wa(1)
+        quantize_wa(2)
+        wo_codes = ring2.tile([P, N], I32, name="wa_grouped", align_bytes=64)
+        nc.sync.dma_start(wo_codes[:], wo_words[0].rearrange("p c i -> p (c i)").bitcast(I32))
+        nc.scalar.copy(gain_wide[:], gain4[:].unsqueeze(2).to_broadcast([P, PACK, HALF]))
+
+        content = [held(f"content{h}", [P, PACK, HALF], F32) for h in range(HALVES)]
+        gate = [held(f"gate{h}", [P, PACK, HALF], F32) for h in range(HALVES)]
+        state = [held(f"state{h}", [P, PACK, HALF], F32) for h in range(HALVES)]
+
+        def first_stage(h):
+            cols = slice(h * HALF, (h + 1) * HALF)
+            b_banks = [psum.tile([P, HALF], F32, name="bank") for t in range(PACK)]
+            a_banks = [psum.tile([P, HALF], F32, name="bank") for t in range(PACK)]
+            for a in range(PASSES):
+                low = v_sc[:, cols] if a == 0 else v_sc_low[:, a - 1, :].bitcast(U8)[:, cols]
+                for t in range(PACK):
+                    nc.tensor.matmul_mx(
+                        out=b_banks[t][:],
+                        lhsT=wb_codes[:, a, :].bitcast(U8)[:, 2 * P * t : 2 * P * (t + 1)].bitcast(FP4X4),
+                        lhsT_scale=wb_sc[:, a, P * t : P * (t + 1)],
+                        rhs=v_codes[a][:, cols].bitcast(FP8X4),
+                        rhs_scale=low,
+                        start=(a == 0),
+                        stop=(a == PASSES - 1),
+                    )
+                for t in range(PACK):
+                    nc.tensor.matmul_mx(
+                        out=a_banks[t][:],
+                        lhsT=wa_codes[a][:, P * t : P * (t + 1)].bitcast(FP8X4),
+                        lhsT_scale=wa_sc[a][:, P * t : P * (t + 1)],
+                        rhs=v_codes[a][:, cols].bitcast(FP8X4),
+                        rhs_scale=v_sc[4 * a :, cols],
+                        start=(a == 0),
+                        stop=(a == PASSES - 1),
+                    )
+            for t in range(PACK):
+                nc.scalar.activation(gate[h][:, t, :], b_banks[t][:], ACT.Sigmoid)
+            for t in range(PACK):
+                nc.scalar.activation(content[h][:, t, :], a_banks[t][:], ACT.Tanh)
+
+        out_rows = out.rearrange("(c p) j -> p c j", p=P)
+
+        def second_stage(h):
+            half_offsets = offsets[:, h * HALF // 16 : (h + 1) * HALF // 16]
+            for t in range(PACK):
+                nc.vector.tensor_tensor(
+                    state[h][:, t, :], g_tab[t][:].indirect(half_offsets), gain_wide[:, t, :], ALU.mult
+                )
+            for t in range(PACK):
+                nc.vector.scalar_tensor_tensor(
+                    content[h][:, t, :], content[h][:, t, :], gain4[:, t : t + 1], gate[h][:, t, :],
+                    ALU.mult, ALU.mult,
+                )
+            for j0 in range(0, HALF, PIECE):
+                cols = slice(j0, j0 + PIECE)
+                h_grouped = ring2.tile([P, PIECE * PACK], BF16, name="h_grouped", align_bytes=64)
+                nc.vector.tensor_tensor(
+                    h_grouped[:].rearrange("p (c i t) -> p c t i", i=4, t=PACK),
+                    content[h][:, :, cols].rearrange("p t (c i) -> p c t i", i=4),
+                    state[h][:, :, cols].rearrange("p t (c i) -> p c t i", i=4),
+                    ALU.add,
+                )
+                h_codes = ring2.tile([P, PIECE], U32, name="h_codes", align_bytes=64)
+                h_sc = ring2.tile([P, PIECE], U8, name="h_sc", align_bytes=64)
+                nc.vector.quantize_mx(out=h_codes[:].bitcast(FP8X4), scales=h_sc[:], in_=h_grouped[:])
+                staged = ring3.tile([P, CHUNKS, PIECE], F32, name="staged")
+                for c0 in range(0, CHUNKS, 2):
+                    bank = psum.tile([P, 2, PIECE], F32, name="bank")
+                    for u in range(2):
+                        n_cols = slice(P * (c0 + u), P * (c0 + u + 1))
+                        nc.tensor.matmul_mx(
+                            out=bank[:, u, :],
+                            lhsT=wo_codes[:, n_cols].bitcast(FP8X4),
+                            lhsT_scale=wo_sc[:].bitcast(U8)[:, n_cols],
+                            rhs=h_codes[:].bitcast(FP8X4),
+                            rhs_scale=h_sc[:],
+                            start=True,
+                            stop=True,
+                        )
+                    if h == HALVES - 1 and j0 + PIECE == HALF and c0 == 2:
+                        nc.vector.tensor_copy(staged[:, c0 : c0 + 2, :], bank[:])
+                    else:
+                        nc.scalar.copy(staged[:, c0 : c0 + 2, :], bank[:])
+                    nc.sync.dma_start(
+                        out_rows[:, c0 : c0 + 2, h * HALF + j0 : h * HALF + j0 + PIECE],
+                        staged[:, c0 : c0 + 2, :],
+                    )
+
+        for h in range(HALVES):
+            first_stage(h)
+        for h in range(HALVES):
+            second_stage(h)

@@ -21,7 +21,7 @@ PACK = 4
 PASSES = K // (P * PACK)
 HALF = 512
 HALVES = S // HALF
-PIECE = 256
+PIECES = ((256, 256), (256, 128, 128))
 CHUNKS = N // P
 QUADS = 4
 SHIFT_ROWS = 112
@@ -46,7 +46,6 @@ def tile_list_gated_neighbor_messages_kernel(
             return keep.tile(shape, dtype, name=name, align_bytes=64)
 
         tab, wa_raw, g_tab = {}, {}, {}
-        wb_raw = held("wb_raw", [P, PASSES, H // 2], I32)
         tab_sc = held("tab_sc", [P, T // 4], I32)
         wb_sc_raw = held("wb_sc_raw", [P, PASSES, H // 4], I32)
         wo_sc = held("wo_sc", [P, N // 4], I32)
@@ -68,6 +67,7 @@ def tile_list_gated_neighbor_messages_kernel(
             nc.sync.dma_start(wa_raw[a][:], rows.rearrange("(p j) c -> p j c", j=PACK))
 
         load_tab(0)
+        wb_raw = big.tile([P, PASSES, H // 2], I32, name="big", align_bytes=64)
         nc.sync.dma_start(wb_raw[:], wb_words.rearrange("a p c -> p a c").bitcast(I32))
         load_tab(1)
         load_wa(0)
@@ -80,7 +80,7 @@ def tile_list_gated_neighbor_messages_kernel(
             nc.sync.dma_start(g_tab[t][:], g_planes[:, t, :])
 
         for q in range(QUADS):
-            nc.gpsimd.dma_start(
+            nc.scalar.dma_start(
                 tab_sc[32 * q : 32 * q + 4 * PASSES, :],
                 tab_scales[:, 4 * q : 4 * q + 4, :].bitcast(I32),
             )
@@ -99,8 +99,8 @@ def tile_list_gated_neighbor_messages_kernel(
         v_sc = held("v_sc", [P, S], U8)
         wa_codes = [held(f"wa_codes{a}", [P, H], U32) for a in range(PASSES)]
         wa_sc = [held(f"wa_sc{a}", [P, H], U8) for a in range(PASSES)]
-        wb_codes = held("wb_codes", [P, PASSES, H // 2], I32)
-        wb_sc = held("wb_sc", [P, PASSES, H], U8)
+        wb_codes = held("wb_codes", [P, PASSES * H // 2], I32)
+        wb_sc = held("wb_sc", [P, PASSES * H], U8)
         gain_wide = held("gain_wide", [P, PACK, HALF], F32)
 
         def gather_words(a):
@@ -121,12 +121,12 @@ def tile_list_gated_neighbor_messages_kernel(
                 v_sc_low[0:SHIFT_ROWS, a - 1, :], v_sc[4 * a : 4 * a + SHIFT_ROWS, :].bitcast(I32)
             )
         nc.vector.tensor_copy(
-            wb_codes[:].bitcast(U16).rearrange("p a (t m) -> p a m t", t=PACK),
-            wb_raw[:].bitcast(U16).rearrange("p a (m t) -> p a m t", t=PACK),
+            wb_codes[:].bitcast(U16).rearrange("p (t c i) -> p c t i", t=PACK, i=8),
+            wb_raw[:].bitcast(U16).rearrange("p a (c i t) -> p (a c) t i", t=PACK, i=8),
         )
         nc.vector.tensor_copy(
-            wb_sc[:].rearrange("p a (t m) -> p a m t", t=PACK),
-            wb_sc_raw[:].bitcast(U8).rearrange("p a (m t) -> p a m t", t=PACK),
+            wb_sc[:].rearrange("p (t c i) -> p c t i", t=PACK, i=16),
+            wb_sc_raw[:].bitcast(U8).rearrange("p a (c i t) -> p (a c) t i", t=PACK, i=16),
         )
         gather_words(1)
         quantize_wa(0)
@@ -148,10 +148,11 @@ def tile_list_gated_neighbor_messages_kernel(
             for a in range(PASSES):
                 low = v_sc[:, cols] if a == 0 else v_sc_low[:, a - 1, :].bitcast(U8)[:, cols]
                 for t in range(PACK):
+                    m0 = P * (PASSES * t + a)
                     nc.tensor.matmul_mx(
                         out=b_banks[t][:],
-                        lhsT=wb_codes[:, a, :].bitcast(U8)[:, 2 * P * t : 2 * P * (t + 1)].bitcast(FP4X4),
-                        lhsT_scale=wb_sc[:, a, P * t : P * (t + 1)],
+                        lhsT=wb_codes[:].bitcast(U8)[:, 2 * m0 : 2 * (m0 + P)].bitcast(FP4X4),
+                        lhsT_scale=wb_sc[:, m0 : m0 + P],
                         rhs=v_codes[a][:, cols].bitcast(FP8X4),
                         rhs_scale=low,
                         start=(a == 0),
@@ -185,22 +186,27 @@ def tile_list_gated_neighbor_messages_kernel(
                     content[h][:, t, :], content[h][:, t, :], gain4[:, t : t + 1], gate[h][:, t, :],
                     ALU.mult, ALU.mult,
                 )
-            for j0 in range(0, HALF, PIECE):
-                cols = slice(j0, j0 + PIECE)
-                h_grouped = ring2.tile([P, PIECE * PACK], BF16, name="h_grouped", align_bytes=64)
+            j0 = 0
+            for width in PIECES[h]:
+                cols = slice(j0, j0 + width)
+                out_cols = slice(h * HALF + j0, h * HALF + j0 + width)
+                j0 += width
+                h_grouped = ring2.tile([P, width * PACK], BF16, name="h_grouped", align_bytes=64)
                 nc.vector.tensor_tensor(
                     h_grouped[:].rearrange("p (c i t) -> p c t i", i=4, t=PACK),
                     content[h][:, :, cols].rearrange("p t (c i) -> p c t i", i=4),
                     state[h][:, :, cols].rearrange("p t (c i) -> p c t i", i=4),
                     ALU.add,
                 )
-                h_codes = ring2.tile([P, PIECE], U32, name="h_codes", align_bytes=64)
-                h_sc = ring2.tile([P, PIECE], U8, name="h_sc", align_bytes=64)
+                h_codes = ring2.tile([P, width], U32, name="h_codes", align_bytes=64)
+                h_sc = ring2.tile([P, width], U8, name="h_sc", align_bytes=64)
                 nc.vector.quantize_mx(out=h_codes[:].bitcast(FP8X4), scales=h_sc[:], in_=h_grouped[:])
-                staged = ring3.tile([P, CHUNKS, PIECE], F32, name="staged")
-                for c0 in range(0, CHUNKS, 2):
-                    bank = psum.tile([P, 2, PIECE], F32, name="bank")
-                    for u in range(2):
+                staged = ring3.tile([P, CHUNKS, width], F32, name="staged")
+                per_bank = min(HALF // width, CHUNKS // 2)
+                for c0 in range(0, CHUNKS, per_bank):
+                    chunks = slice(c0, c0 + per_bank)
+                    bank = psum.tile([P, per_bank, width], F32, name="bank")
+                    for u in range(per_bank):
                         n_cols = slice(P * (c0 + u), P * (c0 + u + 1))
                         nc.tensor.matmul_mx(
                             out=bank[:, u, :],
@@ -211,14 +217,11 @@ def tile_list_gated_neighbor_messages_kernel(
                             start=True,
                             stop=True,
                         )
-                    if h == HALVES - 1 and j0 + PIECE == HALF and c0 == 2:
-                        nc.vector.tensor_copy(staged[:, c0 : c0 + 2, :], bank[:])
+                    if out_cols.stop == S and chunks.stop == CHUNKS:
+                        nc.vector.tensor_copy(staged[:, chunks, :], bank[:])
                     else:
-                        nc.scalar.copy(staged[:, c0 : c0 + 2, :], bank[:])
-                    nc.sync.dma_start(
-                        out_rows[:, c0 : c0 + 2, h * HALF + j0 : h * HALF + j0 + PIECE],
-                        staged[:, c0 : c0 + 2, :],
-                    )
+                        nc.scalar.copy(staged[:, chunks, :], bank[:])
+                    nc.sync.dma_start(out_rows[:, chunks, out_cols], staged[:, chunks, :])
 
         for h in range(HALVES):
             first_stage(h)

@@ -35,7 +35,6 @@ def tile_list_gated_neighbor_messages_kernel(
         lists = ctx.enter_context(tc.tile_pool(name="lists", bufs=1))
         keep = ctx.enter_context(tc.tile_pool(name="keep", bufs=1))
         ring2 = ctx.enter_context(tc.tile_pool(name="ring2", bufs=2))
-        big = ctx.enter_context(tc.tile_pool(name="big", bufs=4))
         ring3 = ctx.enter_context(tc.tile_pool(name="ring3", bufs=3))
         psum = ctx.enter_context(tc.psum_pool(name="psum", bufs=8))
 
@@ -46,7 +45,7 @@ def tile_list_gated_neighbor_messages_kernel(
             return keep.tile(shape, dtype, name=name, align_bytes=64)
 
         tab, wa_raw, g_tab = {}, {}, {}
-        tab_sc = held("tab_sc", [P, T // 4], I32)
+        tab_sc = held("slot_e", [P, T // 4], I32)
         wb_sc_raw = held("wb_sc_raw", [P, PASSES, H // 4], I32)
         wo_sc = held("wo_sc", [P, N // 4], I32)
         v_sc_low = held("v_sc_low", [P, PASSES - 1, S // 4], I32)
@@ -55,28 +54,31 @@ def tile_list_gated_neighbor_messages_kernel(
         nc.vector.memset(tab_sc[:], 0)
         nc.vector.memset(wb_sc_raw[:], 0)
         nc.vector.memset(wo_sc[:], 0)
+        warm_in = held("warm_in", [P, 8], F32)
+        warm_out = held("warm_out", [P, 8], F32)
+        nc.vector.memset(warm_in[:], 0.0)
         nc.vector.memset(v_sc_low[:], 0)
 
-        def load_tab(a):
-            tab[a] = big.tile([P, T], I32, name="big", align_bytes=64)
+        def load_tab(a, slot):
+            tab[a] = held(slot, [P, T], I32)
             nc.sync.dma_start(tab[a][:], tab_words[a].rearrange("p n i -> p (n i)").bitcast(I32))
 
-        def load_wa(a):
+        def load_wa(a, slot):
             rows = wa[a * P * PACK : (a + 1) * P * PACK, :]
-            wa_raw[a] = big.tile([P, PACK, H], F32, name="big", align_bytes=64)
+            wa_raw[a] = held(slot, [P, PACK, H], F32)
             nc.sync.dma_start(wa_raw[a][:], rows.rearrange("(p j) c -> p j c", j=PACK))
 
-        load_tab(0)
-        wb_raw = big.tile([P, PASSES, H // 2], I32, name="big", align_bytes=64)
+        load_tab(0, "slot_a")
+        wb_raw = held("slot_b", [P, PASSES, H // 2], I32)
         nc.sync.dma_start(wb_raw[:], wb_words.rearrange("a p c -> p a c").bitcast(I32))
-        load_tab(1)
-        load_wa(0)
-        load_tab(2)
-        load_wa(1)
-        load_wa(2)
+        load_tab(1, "slot_c")
+        load_wa(0, "slot_d")
+        load_tab(2, "slot_a")
+        load_wa(1, "slot_b")
+        load_wa(2, "slot_e")
         g_planes = gT.rearrange("(p t) n -> p t n", t=PACK)
-        for t in range(PACK):
-            g_tab[t] = big.tile([P, T], F32, name="big", align_bytes=64)
+        for t, slot in enumerate(("slot_d", "slot_c", "slot_b")):
+            g_tab[t] = held(slot, [P, T], F32)
             nc.sync.dma_start(g_tab[t][:], g_planes[:, t, :])
 
         for q in range(QUADS):
@@ -95,6 +97,7 @@ def tile_list_gated_neighbor_messages_kernel(
                 wo_sc[32 * q : 32 * q + 4, :], wo_scales[0, 4 * q : 4 * q + 4, :].bitcast(I32)
             )
 
+        nc.scalar.activation(warm_out[:], warm_in[:], ACT.Sigmoid)
         v_codes = [held(f"v_codes{a}", [P, S], U32) for a in range(PASSES)]
         v_sc = held("v_sc", [P, S], U8)
         wa_codes = [held(f"wa_codes{a}", [P, H], U32) for a in range(PASSES)]
@@ -133,12 +136,14 @@ def tile_list_gated_neighbor_messages_kernel(
         gather_words(2)
         quantize_wa(1)
         quantize_wa(2)
+        g_tab[3] = ring2.tile([P, T], F32, name="wa_grouped", align_bytes=64)
+        nc.sync.dma_start(g_tab[3][:], g_planes[:, 3, :])
         wo_codes = ring2.tile([P, N], I32, name="wa_grouped", align_bytes=64)
         nc.sync.dma_start(wo_codes[:], wo_words[0].rearrange("p c i -> p (c i)").bitcast(I32))
         nc.scalar.copy(gain_wide[:], gain4[:].unsqueeze(2).to_broadcast([P, PACK, HALF]))
 
         content = [held(f"content{h}", [P, PACK, HALF], F32) for h in range(HALVES)]
-        gate = [held(f"gate{h}", [P, PACK, HALF], F32) for h in range(HALVES)]
+        gate = [held(slot, [P, PACK, HALF], F32) for slot in ("slot_e", "gate1")]
         state = [held(f"state{h}", [P, PACK, HALF], F32) for h in range(HALVES)]
 
         def first_stage(h):

@@ -111,10 +111,11 @@ def tile_list_gated_neighbor_messages_kernel(
 
         def quantize_wa(a):
             grouped = ring2.tile([P, H * PACK], BF16, name="wa_grouped", align_bytes=64)
-            nc.scalar.copy(
-                grouped[:].rearrange("p (t m j) -> p m j t", t=PACK, j=PACK),
-                wa_raw[a][:].rearrange("p j (m t) -> p m j t", t=PACK),
-            )
+            for t0 in range(0, PACK, 2):
+                nc.scalar.copy(
+                    grouped[:].rearrange("p (t m j) -> p m j t", t=PACK, j=PACK)[:, :, :, t0 : t0 + 2],
+                    wa_raw[a][:].rearrange("p j (m t) -> p m j t", t=PACK)[:, :, :, t0 : t0 + 2],
+                )
             nc.vector.quantize_mx(out=wa_codes[a][:].bitcast(FP8X4), scales=wa_sc[a][:], in_=grouped[:])
 
         gather_words(0)
@@ -182,15 +183,20 @@ def tile_list_gated_neighbor_messages_kernel(
 
         def second_stage(h):
             half_offsets = offsets[:, h * HALF // 16 : (h + 1) * HALF // 16]
-            for t in range(PACK):
+
+            def gather_state(t):
                 nc.vector.tensor_tensor(
                     state[h][:, t, :], g_tab[t][:].indirect(half_offsets), gain_wide[:, t, :], ALU.mult
                 )
+
+            for t in range(PACK - 1):
+                gather_state(t)
             for t in range(PACK):
                 nc.vector.scalar_tensor_tensor(
                     content[h][:, t, :], content[h][:, t, :], gain4[:, t : t + 1], gate[h][:, t, :],
                     ALU.mult, ALU.mult,
                 )
+            gather_state(PACK - 1)
             j0 = 0
             for width in PIECES[h]:
                 cols = slice(j0, j0 + width)
@@ -198,9 +204,9 @@ def tile_list_gated_neighbor_messages_kernel(
                 j0 += width
                 h_grouped = ring2.tile([P, width * PACK], BF16, name="h_grouped", align_bytes=64)
                 nc.vector.tensor_tensor(
-                    h_grouped[:].rearrange("p (c i t) -> p c t i", i=4, t=PACK),
-                    content[h][:, :, cols].rearrange("p t (c i) -> p c t i", i=4),
-                    state[h][:, :, cols].rearrange("p t (c i) -> p c t i", i=4),
+                    h_grouped[:].rearrange("p (c i t) -> p c t i", i=2, t=PACK),
+                    content[h][:, :, cols].rearrange("p t (c i) -> p c t i", i=2),
+                    state[h][:, :, cols].rearrange("p t (c i) -> p c t i", i=2),
                     ALU.add,
                 )
                 h_codes = ring2.tile([P, width], U32, name="h_codes", align_bytes=64)

@@ -21,10 +21,12 @@ PACK = 4
 PASSES = K // (P * PACK)
 HALF = 512
 HALVES = S // HALF
-PIECES = ((256, 256), (256, 128, 128))
 CHUNKS = N // P
 QUADS = 4
+LIST_ROWS = 16
 SHIFT_ROWS = 112
+FIRST_GROUP = (0, (256, 256), (0, 1, 2, 3))
+LATER_GROUPS = ((512, (256,), (3,)), (768, (128, 128), (3,)))
 
 
 def tile_list_gated_neighbor_messages_kernel(
@@ -38,15 +40,14 @@ def tile_list_gated_neighbor_messages_kernel(
         ring3 = ctx.enter_context(tc.tile_pool(name="ring3", bufs=3))
         psum = ctx.enter_context(tc.psum_pool(name="psum", bufs=8))
 
-        offsets = lists.tile([P, S // 16], U16, name="offsets")
-        nc.sync.dma_start(offsets[:], offs)
+        offsets = lists.tile([P, S // LIST_ROWS], U16, name="offsets")
 
         def held(name, shape, dtype):
             return keep.tile(shape, dtype, name=name, align_bytes=64)
 
         tab, wa_raw, g_tab = {}, {}, {}
         tab_sc = held("slot_e", [P, T // 4], I32)
-        wb_sc_raw = held("wb_sc_raw", [P, PASSES, H // 4], I32)
+        wb_sc_raw = held("slot_f", [P, PASSES, H // 4], I32)
         wo_sc = held("wo_sc", [P, N // 4], I32)
         v_sc_low = held("v_sc_low", [P, PASSES - 1, S // 4], I32)
         gain4 = held("gain4", [P, PACK], F32)
@@ -68,6 +69,7 @@ def tile_list_gated_neighbor_messages_kernel(
             wa_raw[a] = held(slot, [P, PACK, H], F32)
             nc.sync.dma_start(wa_raw[a][:], rows.rearrange("(p j) c -> p j c", j=PACK))
 
+        nc.sync.dma_start(offsets[:], offs)
         load_tab(0, "slot_a")
         wb_raw = held("slot_b", [P, PASSES, H // 2], I32)
         nc.sync.dma_start(wb_raw[:], wb_words.rearrange("a p c -> p a c").bitcast(I32))
@@ -77,7 +79,7 @@ def tile_list_gated_neighbor_messages_kernel(
         load_wa(1, "slot_b")
         load_wa(2, "slot_e")
         g_planes = gT.rearrange("(p t) n -> p t n", t=PACK)
-        for t, slot in enumerate(("slot_d", "slot_c", "slot_b")):
+        for t, slot in enumerate(("slot_d", "slot_f", "slot_b")):
             g_tab[t] = held(slot, [P, T], F32)
             nc.sync.dma_start(g_tab[t][:], g_planes[:, t, :])
 
@@ -98,19 +100,20 @@ def tile_list_gated_neighbor_messages_kernel(
             )
 
         nc.scalar.activation(warm_out[:], warm_in[:], ACT.Sigmoid)
+
         v_codes = [held(f"v_codes{a}", [P, S], U32) for a in range(PASSES)]
         v_sc = held("v_sc", [P, S], U8)
         wa_codes = [held(f"wa_codes{a}", [P, H], U32) for a in range(PASSES)]
         wa_sc = [held(f"wa_sc{a}", [P, H], U8) for a in range(PASSES)]
         wb_codes = held("wb_codes", [P, PASSES * H // 2], I32)
-        wb_sc = held("wb_sc", [P, PASSES * H], U8)
+        wb_sc = held("slot_c", [P, PASSES * H], U8)
         gain_wide = held("gain_wide", [P, PACK, HALF], F32)
 
         def gather_words(a):
             nc.vector.tensor_copy(v_codes[a][:], tab[a][:].bitcast(U32).indirect(offsets[:]))
 
         def quantize_wa(a):
-            grouped = ring2.tile([P, H * PACK], BF16, name="wa_grouped", align_bytes=64)
+            grouped = ring2.tile([P, H * PACK], BF16, name="wa_ring", align_bytes=64)
             for t0 in range(0, PACK, 2):
                 nc.scalar.copy(
                     grouped[:].rearrange("p (t m j) -> p m j t", t=PACK, j=PACK)[:, :, :, t0 : t0 + 2],
@@ -119,33 +122,34 @@ def tile_list_gated_neighbor_messages_kernel(
             nc.vector.quantize_mx(out=wa_codes[a][:].bitcast(FP8X4), scales=wa_sc[a][:], in_=grouped[:])
 
         gather_words(0)
+        nc.vector.tensor_copy(
+            wb_codes[:].bitcast(U16).rearrange("p (t c i) -> p c t i", t=PACK, i=8),
+            wb_raw[:].bitcast(U16).rearrange("p a (c i t) -> p (a c) t i", t=PACK, i=8),
+        )
+        gather_words(1)
         nc.vector.tensor_copy(v_sc[:], tab_sc[:].bitcast(U8).indirect(offsets[:]))
         for a in range(1, PASSES):
             nc.scalar.dma_start(
                 v_sc_low[0:SHIFT_ROWS, a - 1, :], v_sc[4 * a : 4 * a + SHIFT_ROWS, :].bitcast(I32)
             )
         nc.vector.tensor_copy(
-            wb_codes[:].bitcast(U16).rearrange("p (t c i) -> p c t i", t=PACK, i=8),
-            wb_raw[:].bitcast(U16).rearrange("p a (c i t) -> p (a c) t i", t=PACK, i=8),
-        )
-        nc.vector.tensor_copy(
             wb_sc[:].rearrange("p (t c i) -> p c t i", t=PACK, i=16),
             wb_sc_raw[:].bitcast(U8).rearrange("p a (c i t) -> p (a c) t i", t=PACK, i=16),
         )
-        gather_words(1)
         quantize_wa(0)
         gather_words(2)
         quantize_wa(1)
         quantize_wa(2)
-        g_tab[3] = ring2.tile([P, T], F32, name="wa_grouped", align_bytes=64)
+        g_tab[3] = ring2.tile([P, T], F32, name="wa_ring", align_bytes=64)
         nc.sync.dma_start(g_tab[3][:], g_planes[:, 3, :])
-        wo_codes = ring2.tile([P, N], I32, name="wa_grouped", align_bytes=64)
+        wo_codes = ring2.tile([P, N], I32, name="wa_ring", align_bytes=64)
         nc.sync.dma_start(wo_codes[:], wo_words[0].rearrange("p c i -> p (c i)").bitcast(I32))
         nc.scalar.copy(gain_wide[:], gain4[:].unsqueeze(2).to_broadcast([P, PACK, HALF]))
 
         content = [held(f"content{h}", [P, PACK, HALF], F32) for h in range(HALVES)]
         gate = [held(slot, [P, PACK, HALF], F32) for slot in ("slot_e", "gate1")]
-        state = [held(f"state{h}", [P, PACK, HALF], F32) for h in range(HALVES)]
+        state_planes = held("state_planes", [P, 2 * PACK - 1, HALF], F32)
+        state = [state_planes[:, PACK - 1 :, :], state_planes[:, :PACK, :]]
 
         def first_stage(h):
             cols = slice(h * HALF, (h + 1) * HALF)
@@ -181,60 +185,77 @@ def tile_list_gated_neighbor_messages_kernel(
 
         out_rows = out.rearrange("(c p) j -> p c j", p=P)
 
-        def second_stage(h):
-            half_offsets = offsets[:, h * HALF // 16 : (h + 1) * HALF // 16]
+        def gather_state(t, j0, width):
+            h, c0 = divmod(j0, HALF)
+            nc.vector.tensor_tensor(
+                state[h][:, t, c0 : c0 + width],
+                g_tab[t][:].indirect(offsets[:, j0 // LIST_ROWS : (j0 + width) // LIST_ROWS]),
+                gain_wide[:, t, :width],
+                ALU.mult,
+            )
 
-            def gather_state(t):
-                nc.vector.tensor_tensor(
-                    state[h][:, t, :], g_tab[t][:].indirect(half_offsets), gain_wide[:, t, :], ALU.mult
-                )
-
-            for t in range(PACK - 1):
-                gather_state(t)
+        def gate_content(j0, width):
+            h, c0 = divmod(j0, HALF)
+            cols = slice(c0, c0 + width)
             for t in range(PACK):
                 nc.vector.scalar_tensor_tensor(
-                    content[h][:, t, :], content[h][:, t, :], gain4[:, t : t + 1], gate[h][:, t, :],
+                    content[0][:, t, cols], content[h][:, t, cols], gain4[:, t : t + 1], gate[h][:, t, cols],
                     ALU.mult, ALU.mult,
                 )
-            gather_state(PACK - 1)
-            j0 = 0
-            for width in PIECES[h]:
-                cols = slice(j0, j0 + width)
-                out_cols = slice(h * HALF + j0, h * HALF + j0 + width)
-                j0 += width
-                h_grouped = ring2.tile([P, width * PACK], BF16, name="h_grouped", align_bytes=64)
-                nc.vector.tensor_tensor(
-                    h_grouped[:].rearrange("p (c i t) -> p c t i", i=2, t=PACK),
-                    content[h][:, :, cols].rearrange("p t (c i) -> p c t i", i=2),
-                    state[h][:, :, cols].rearrange("p t (c i) -> p c t i", i=2),
-                    ALU.add,
-                )
-                h_codes = ring2.tile([P, width], U32, name="h_codes", align_bytes=64)
-                h_sc = ring2.tile([P, width], U8, name="h_sc", align_bytes=64)
-                nc.vector.quantize_mx(out=h_codes[:].bitcast(FP8X4), scales=h_sc[:], in_=h_grouped[:])
-                staged = ring3.tile([P, CHUNKS, width], F32, name="staged")
-                per_bank = min(HALF // width, CHUNKS // 2)
-                for c0 in range(0, CHUNKS, per_bank):
-                    chunks = slice(c0, c0 + per_bank)
-                    bank = psum.tile([P, per_bank, width], F32, name="bank")
-                    for u in range(per_bank):
-                        n_cols = slice(P * (c0 + u), P * (c0 + u + 1))
-                        nc.tensor.matmul_mx(
-                            out=bank[:, u, :],
-                            lhsT=wo_codes[:, n_cols].bitcast(FP8X4),
-                            lhsT_scale=wo_sc[:].bitcast(U8)[:, n_cols],
-                            rhs=h_codes[:].bitcast(FP8X4),
-                            rhs_scale=h_sc[:],
-                            start=True,
-                            stop=True,
-                        )
-                    if out_cols.stop == S and chunks.stop == CHUNKS:
-                        nc.vector.tensor_copy(staged[:, chunks, :], bank[:])
-                    else:
-                        nc.scalar.copy(staged[:, chunks, :], bank[:])
-                    nc.sync.dma_start(out_rows[:, chunks, out_cols], staged[:, chunks, :])
+
+        def quantize_h(j0, width):
+            h, c0 = divmod(j0, HALF)
+            cols = slice(c0, c0 + width)
+            h_grouped = ring2.tile([P, width * PACK], BF16, name="h_grouped", align_bytes=64)
+            nc.vector.tensor_tensor(
+                h_grouped[:].rearrange("p (c i t) -> p c t i", i=2, t=PACK),
+                content[0][:, :, cols].rearrange("p t (c i) -> p c t i", i=2),
+                state[h][:, :, cols].rearrange("p t (c i) -> p c t i", i=2),
+                ALU.add,
+            )
+            h_codes = ring2.tile([P, width], U32, name="h_codes", align_bytes=64)
+            h_sc = ring2.tile([P, width], U8, name="h_sc", align_bytes=64)
+            nc.vector.quantize_mx(out=h_codes[:].bitcast(FP8X4), scales=h_sc[:], in_=h_grouped[:])
+            return h_codes, h_sc
+
+        def project(j0, width, h_codes, h_sc, share_copies):
+            staged = ring3.tile([P, CHUNKS, width], F32, name="staged")
+            per_bank = min(HALF // width, CHUNKS // 2)
+            for c0 in range(0, CHUNKS, per_bank):
+                chunks = slice(c0, c0 + per_bank)
+                bank = psum.tile([P, per_bank, width], F32, name="bank")
+                for u in range(per_bank):
+                    n_cols = slice(P * (c0 + u), P * (c0 + u + 1))
+                    nc.tensor.matmul_mx(
+                        out=bank[:, u, :],
+                        lhsT=wo_codes[:, n_cols].bitcast(FP8X4),
+                        lhsT_scale=wo_sc[:].bitcast(U8)[:, n_cols],
+                        rhs=h_codes[:].bitcast(FP8X4),
+                        rhs_scale=h_sc[:],
+                        start=True,
+                        stop=True,
+                    )
+                if share_copies and c0 > 0:
+                    nc.vector.tensor_copy(staged[:, chunks, :], bank[:])
+                else:
+                    nc.scalar.copy(staged[:, chunks, :], bank[:])
+                nc.sync.dma_start(out_rows[:, chunks, j0 : j0 + width], staged[:, chunks, :])
+
+        def second_stage(j0, widths, planes):
+            total = sum(widths)
+            for t in planes[:-1]:
+                gather_state(t, j0, total)
+            gate_content(j0, total)
+            gather_state(planes[-1], j0, total)
+            starts = [j0 + sum(widths[:i]) for i in range(len(widths))]
+            operands = [quantize_h(start, width) for start, width in zip(starts, widths)]
+            for start, width, (h_codes, h_sc) in zip(starts, widths, operands):
+                project(start, width, h_codes, h_sc, share_copies=(j0 + total == S))
 
         for h in range(HALVES):
             first_stage(h)
-        for h in range(HALVES):
-            second_stage(h)
+        second_stage(*FIRST_GROUP)
+        for t in range(PACK - 1):
+            gather_state(t, HALF, HALF)
+        for group in LATER_GROUPS:
+            second_stage(*group)

@@ -25,8 +25,8 @@ CHUNKS = N // P
 QUADS = 4
 LIST_ROWS = 16
 SHIFT_ROWS = 112
-FIRST_GROUP = (0, (256, 256), (0, 1, 2, 3))
-LATER_GROUPS = ((512, (256,), (3,)), (768, (128, 128), (3,)))
+GROUPS = ((0, (256,)), (256, (256,)), (512, (256,)), (768, (128, 128)))
+KIB = 1024
 
 
 def tile_list_gated_neighbor_messages_kernel(
@@ -40,80 +40,91 @@ def tile_list_gated_neighbor_messages_kernel(
         ring3 = ctx.enter_context(tc.tile_pool(name="ring3", bufs=3))
         psum = ctx.enter_context(tc.psum_pool(name="psum", bufs=8))
 
+        placed = ctx.enter_context(tc.tile_pool(name="placed", bufs=1))
         offsets = lists.tile([P, S // LIST_ROWS], U16, name="offsets")
 
         def held(name, shape, dtype):
             return keep.tile(shape, dtype, name=name, align_bytes=64)
 
+        def place(name, shape, dtype, at):
+            return placed.tile(shape, dtype, name=name, align_bytes=64, offset=at)
+
+        at_tab2, at_wb, at_wa0, at_tab0 = 0, 7 * KIB, 9 * KIB + 512, 18 * KIB
+        at_codes1, at_tab_sc, at_g0 = 26 * KIB, 29 * KIB, 30 * KIB
+        at_wa1, at_tab1, at_wb_sc = 40 * KIB, 46 * KIB, 52 * KIB + 512
+        at_codes2, at_wb_sc_raw, at_wa2 = 54 * KIB + 512, 58 * KIB, 58 * KIB + 512
+        at_cast = (67 * KIB, 75 * KIB, 79 * KIB)
         tab, wa_raw, g_tab = {}, {}, {}
-        tab_sc = held("slot_e", [P, T // 4], I32)
-        wb_sc_raw = held("slot_f", [P, PASSES, H // 4], I32)
+        tab_sc = place("tab_sc", [P, T // 4], I32, at_tab_sc)
+        wb_sc_raw = place("wb_sc_raw", [P, PASSES, H // 4], I32, at_wb_sc_raw)
         wo_sc = held("wo_sc", [P, N // 4], I32)
         v_sc_low = held("v_sc_low", [P, PASSES - 1, S // 4], I32)
         gain4 = held("gain4", [P, PACK], F32)
 
         nc.vector.memset(tab_sc[:], 0)
         nc.vector.memset(wb_sc_raw[:], 0)
-        nc.vector.memset(wo_sc[:], 0)
         warm_in = held("warm_in", [P, 8], F32)
         warm_out = held("warm_out", [P, 8], F32)
         nc.vector.memset(warm_in[:], 0.0)
         nc.vector.memset(v_sc_low[:], 0)
 
-        def load_tab(a, slot):
-            tab[a] = held(slot, [P, T], I32)
+        def load_tab(a, at):
+            tab[a] = place(f"tab{a}", [P, T], I32, at)
             nc.sync.dma_start(tab[a][:], tab_words[a].rearrange("p n i -> p (n i)").bitcast(I32))
 
-        def load_wa(a, slot):
+        def load_wa(a, at):
             rows = wa[a * P * PACK : (a + 1) * P * PACK, :]
-            wa_raw[a] = held(slot, [P, PACK, H], F32)
+            wa_raw[a] = place(f"wa_raw{a}", [P, PACK, H], F32, at)
             nc.sync.dma_start(wa_raw[a][:], rows.rearrange("(p j) c -> p j c", j=PACK))
 
-        nc.sync.dma_start(offsets[:], offs)
-        load_tab(0, "slot_a")
-        wb_raw = held("slot_b", [P, PASSES, H // 2], I32)
-        nc.sync.dma_start(wb_raw[:], wb_words.rearrange("a p c -> p a c").bitcast(I32))
-        load_tab(1, "slot_c")
-        load_wa(0, "slot_d")
-        load_tab(2, "slot_a")
-        load_wa(1, "slot_b")
-        load_wa(2, "slot_e")
         g_planes = gT.rearrange("(p t) n -> p t n", t=PACK)
-        for t, slot in enumerate(("slot_d", "slot_f", "slot_b")):
-            g_tab[t] = held(slot, [P, T], F32)
+
+        def load_g(t, at):
+            g_tab[t] = place(f"g_tab{t}", [P, T], F32, at)
             nc.sync.dma_start(g_tab[t][:], g_planes[:, t, :])
 
+        nc.sync.dma_start(offsets[:], offs)
+        wb_raw = place("wb_raw", [P, PASSES, H // 2], I32, at_wb)
+        nc.sync.dma_start(wb_raw[:], wb_words.rearrange("a p c -> p a c").bitcast(I32))
+        load_tab(0, at_tab0)
+        load_tab(1, at_tab1)
         for q in range(QUADS):
-            nc.scalar.dma_start(
+            (nc.scalar, nc.sync)[q % 2].dma_start(
                 tab_sc[32 * q : 32 * q + 4 * PASSES, :],
                 tab_scales[:, 4 * q : 4 * q + 4, :].bitcast(I32),
             )
         for q in range(QUADS):
-            nc.scalar.dma_start(
+            nc.gpsimd.dma_start(
                 wb_sc_raw[32 * q : 32 * q + 4, :, :],
                 wb_scales[:, 4 * q : 4 * q + 4, :].rearrange("a r c -> r a c").bitcast(I32),
             )
         nc.gpsimd.dma_start(gain4[:], gain.rearrange("(p t) -> p t", t=PACK))
+        nc.vector.memset(wo_sc[:], 0)
         for q in range(QUADS):
             nc.gpsimd.dma_start(
                 wo_sc[32 * q : 32 * q + 4, :], wo_scales[0, 4 * q : 4 * q + 4, :].bitcast(I32)
             )
+        load_tab(2, at_tab2)
+        load_wa(0, at_wa0)
 
         nc.scalar.activation(warm_out[:], warm_in[:], ACT.Sigmoid)
 
-        v_codes = [held(f"v_codes{a}", [P, S], U32) for a in range(PASSES)]
-        v_sc = held("v_sc", [P, S], U8)
+        v_codes = [
+            held("v_codes0", [P, S], U32),
+            place("v_codes1", [P, S], U32, at_codes1),
+            place("v_codes2", [P, S], U32, at_codes2),
+        ]
+        v_sc = place("v_sc", [P, S], U8, at_tab0)
         wa_codes = [held(f"wa_codes{a}", [P, H], U32) for a in range(PASSES)]
         wa_sc = [held(f"wa_sc{a}", [P, H], U8) for a in range(PASSES)]
         wb_codes = held("wb_codes", [P, PASSES * H // 2], I32)
-        wb_sc = held("slot_c", [P, PASSES * H], U8)
-        gain_wide = held("gain_wide", [P, PACK, HALF], F32)
+        wb_sc = place("wb_sc", [P, PASSES * H], U8, at_wb_sc)
 
         def gather_words(a):
             nc.vector.tensor_copy(v_codes[a][:], tab[a][:].bitcast(U32).indirect(offsets[:]))
 
         def quantize_wa(a):
-            grouped = ring2.tile([P, H * PACK], BF16, name="wa_ring", align_bytes=64)
+            grouped = place(f"grouped{a}", [P, H * PACK], BF16, at_cast[a])
             for t0 in range(0, PACK, 2):
                 nc.scalar.copy(
                     grouped[:].rearrange("p (t m j) -> p m j t", t=PACK, j=PACK)[:, :, :, t0 : t0 + 2],
@@ -121,35 +132,39 @@ def tile_list_gated_neighbor_messages_kernel(
                 )
             nc.vector.quantize_mx(out=wa_codes[a][:].bitcast(FP8X4), scales=wa_sc[a][:], in_=grouped[:])
 
-        gather_words(0)
         nc.vector.tensor_copy(
             wb_codes[:].bitcast(U16).rearrange("p (t c i) -> p c t i", t=PACK, i=8),
             wb_raw[:].bitcast(U16).rearrange("p a (c i t) -> p (a c) t i", t=PACK, i=8),
         )
-        gather_words(1)
+        gather_words(0)
         nc.vector.tensor_copy(v_sc[:], tab_sc[:].bitcast(U8).indirect(offsets[:]))
         for a in range(1, PASSES):
             nc.scalar.dma_start(
                 v_sc_low[0:SHIFT_ROWS, a - 1, :], v_sc[4 * a : 4 * a + SHIFT_ROWS, :].bitcast(I32)
             )
+        load_wa(1, at_g0)
+        gather_words(1)
+        load_wa(2, at_wa1)
         nc.vector.tensor_copy(
             wb_sc[:].rearrange("p (t c i) -> p c t i", t=PACK, i=16),
             wb_sc_raw[:].bitcast(U8).rearrange("p a (c i t) -> p (a c) t i", t=PACK, i=16),
         )
-        quantize_wa(0)
+        load_g(0, at_wa2)
         gather_words(2)
+        load_g(1, at_tab2)
+        quantize_wa(0)
+        load_g(2, at_wa0)
+        load_g(3, at_cast[0])
         quantize_wa(1)
         quantize_wa(2)
-        g_tab[3] = ring2.tile([P, T], F32, name="wa_ring", align_bytes=64)
-        nc.sync.dma_start(g_tab[3][:], g_planes[:, 3, :])
-        wo_codes = ring2.tile([P, N], I32, name="wa_ring", align_bytes=64)
+        wo_codes = place("wo_codes", [P, N], I32, at_g0)
         nc.sync.dma_start(wo_codes[:], wo_words[0].rearrange("p c i -> p (c i)").bitcast(I32))
-        nc.scalar.copy(gain_wide[:], gain4[:].unsqueeze(2).to_broadcast([P, PACK, HALF]))
 
         content = [held(f"content{h}", [P, PACK, HALF], F32) for h in range(HALVES)]
-        gate = [held(slot, [P, PACK, HALF], F32) for slot in ("slot_e", "gate1")]
-        state_planes = held("state_planes", [P, 2 * PACK - 1, HALF], F32)
-        state = [state_planes[:, PACK - 1 :, :], state_planes[:, :PACK, :]]
+        gate = [place("gate0", [P, PACK, HALF], F32, at_wa1), held("gate1", [P, PACK, HALF], F32)]
+        state = [held(f"state{h}", [P, PACK, HALF], F32) for h in range(HALVES)]
+        gain_wide = held("gain_wide", [P, PACK, HALF], F32)
+        nc.scalar.copy(gain_wide[:], gain4[:].unsqueeze(2).to_broadcast([P, PACK, HALF]))
 
         def first_stage(h):
             cols = slice(h * HALF, (h + 1) * HALF)
@@ -197,19 +212,21 @@ def tile_list_gated_neighbor_messages_kernel(
         def gate_content(j0, width):
             h, c0 = divmod(j0, HALF)
             cols = slice(c0, c0 + width)
+            gated = held("gated", [P, PACK, width], F32)
             for t in range(PACK):
                 nc.vector.scalar_tensor_tensor(
-                    content[0][:, t, cols], content[h][:, t, cols], gain4[:, t : t + 1], gate[h][:, t, cols],
+                    gated[:, t, :], content[h][:, t, cols], gain4[:, t : t + 1], gate[h][:, t, cols],
                     ALU.mult, ALU.mult,
                 )
+            return gated
 
-        def quantize_h(j0, width):
+        def quantize_h(gated, g0, j0, width):
             h, c0 = divmod(j0, HALF)
             cols = slice(c0, c0 + width)
             h_grouped = ring2.tile([P, width * PACK], BF16, name="h_grouped", align_bytes=64)
             nc.vector.tensor_tensor(
                 h_grouped[:].rearrange("p (c i t) -> p c t i", i=2, t=PACK),
-                content[0][:, :, cols].rearrange("p t (c i) -> p c t i", i=2),
+                gated[:, :, j0 - g0 : j0 - g0 + width].rearrange("p t (c i) -> p c t i", i=2),
                 state[h][:, :, cols].rearrange("p t (c i) -> p c t i", i=2),
                 ALU.add,
             )
@@ -241,21 +258,19 @@ def tile_list_gated_neighbor_messages_kernel(
                     nc.scalar.copy(staged[:, chunks, :], bank[:])
                 nc.sync.dma_start(out_rows[:, chunks, j0 : j0 + width], staged[:, chunks, :])
 
-        def second_stage(j0, widths, planes):
+        def second_stage(j0, widths):
             total = sum(widths)
-            for t in planes[:-1]:
-                gather_state(t, j0, total)
-            gate_content(j0, total)
-            gather_state(planes[-1], j0, total)
+            gated = gate_content(j0, total)
+            gather_state(PACK - 1, j0, total)
             starts = [j0 + sum(widths[:i]) for i in range(len(widths))]
-            operands = [quantize_h(start, width) for start, width in zip(starts, widths)]
+            operands = [quantize_h(gated, j0, start, width) for start, width in zip(starts, widths)]
             for start, width, (h_codes, h_sc) in zip(starts, widths, operands):
                 project(start, width, h_codes, h_sc, share_copies=(j0 + total == S))
 
         for h in range(HALVES):
             first_stage(h)
-        second_stage(*FIRST_GROUP)
         for t in range(PACK - 1):
-            gather_state(t, HALF, HALF)
-        for group in LATER_GROUPS:
+            for h in range(HALVES):
+                gather_state(t, h * HALF, HALF)
+        for group in GROUPS:
             second_stage(*group)

@@ -163,8 +163,8 @@ def tile_list_gated_neighbor_messages_kernel(
         content = [held(f"content{h}", [P, PACK, HALF], F32) for h in range(HALVES)]
         gate = [place("gate0", [P, PACK, HALF], F32, at_wa1), held("gate1", [P, PACK, HALF], F32)]
         state = [held(f"state{h}", [P, PACK, HALF], F32) for h in range(HALVES)]
-        gain_wide = held("gain_wide", [P, PACK, HALF], F32)
-        nc.scalar.copy(gain_wide[:], gain4[:].unsqueeze(2).to_broadcast([P, PACK, HALF]))
+        gain_wide = held("gain_wide", [P, HALF // 2], F32)
+        nc.scalar.copy(gain_wide[:], gain4[:, PACK - 1 :].to_broadcast([P, HALF // 2]))
 
         def first_stage(h):
             cols = slice(h * HALF, (h + 1) * HALF)
@@ -205,7 +205,7 @@ def tile_list_gated_neighbor_messages_kernel(
             nc.vector.tensor_tensor(
                 state[h][:, t, c0 : c0 + width],
                 g_tab[t][:].indirect(offsets[:, j0 // LIST_ROWS : (j0 + width) // LIST_ROWS]),
-                gain_wide[:, t, :width],
+                gain_wide[:, :width],
                 ALU.mult,
             )
 
@@ -270,7 +270,11 @@ def tile_list_gated_neighbor_messages_kernel(
         for h in range(HALVES):
             first_stage(h)
         for t in range(PACK - 1):
+            picked = held(f"picked{t}", [P, S], F32)
+            nc.vector.tensor_copy(picked[:], g_tab[t][:].indirect(offsets[:]))
             for h in range(HALVES):
-                gather_state(t, h * HALF, HALF)
+                nc.scalar.activation(
+                    state[h][:, t, :], picked[:, h * HALF : (h + 1) * HALF], ACT.Copy, scale=gain4[:, t : t + 1]
+                )
         for group in GROUPS:
             second_stage(*group)

@@ -25,8 +25,9 @@ CHUNKS = N // P
 QUADS = 4
 LIST_ROWS = 16
 SHIFT_ROWS = 112
-GROUPS = ((0, (256,)), (256, (256,)), (512, (256,)), (768, (128, 128)))
+PIECES = (256, 256, 256, 128, 128)
 KIB = 1024
+LAP = 64
 
 
 def tile_list_gated_neighbor_messages_kernel(
@@ -39,7 +40,6 @@ def tile_list_gated_neighbor_messages_kernel(
         ring2 = ctx.enter_context(tc.tile_pool(name="ring2", bufs=2))
         ring3 = ctx.enter_context(tc.tile_pool(name="ring3", bufs=3))
         psum = ctx.enter_context(tc.psum_pool(name="psum", bufs=8))
-
         placed = ctx.enter_context(tc.tile_pool(name="placed", bufs=1))
         offsets = lists.tile([P, S // LIST_ROWS], U16, name="offsets")
 
@@ -49,193 +49,213 @@ def tile_list_gated_neighbor_messages_kernel(
         def place(name, shape, dtype, at):
             return placed.tile(shape, dtype, name=name, align_bytes=64, offset=at)
 
-        at_tab2, at_wb, at_wa0, at_tab0 = 0, 7 * KIB, 9 * KIB + 512, 18 * KIB
-        at_codes1, at_tab_sc, at_g0 = 26 * KIB, 29 * KIB, 30 * KIB
-        at_wa1, at_tab1, at_wb_sc = 40 * KIB, 46 * KIB, 52 * KIB + 512
-        at_codes2, at_wb_sc_raw, at_wa2 = 54 * KIB + 512, 58 * KIB, 58 * KIB + 512
-        at_cast = (67 * KIB, 75 * KIB, 79 * KIB)
-        tab, wa_raw, g_tab = {}, {}, {}
+        at_tab = (62 * KIB - LAP, 87 * KIB - LAP, 0)
+        at_wa = (11 * KIB - 2 * LAP, 36 * KIB, 45 * KIB + 512 - 2 * LAP)
+        at_g = (54 * KIB, 70 * KIB - 2 * LAP, 79 * KIB, 95 * KIB - 2 * LAP)
+        at_wb_raw, at_wb_sc, at_wb_sc_raw = 8 * KIB - LAP, 8 * KIB + LAP, 44 * KIB - LAP
+        at_gate, at_v_sc, at_wo = 19 * KIB - 3 * LAP, 63 * KIB, 0
+        at_tab_sc, at_codes2 = 104 * KIB, (103 * KIB + 512, 105 * KIB + 512)
+        at_state, at_wa_codes2 = (108 * KIB, 118 * KIB - 2 * LAP), 116 * KIB - LAP
+
         tab_sc = place("tab_sc", [P, T // 4], I32, at_tab_sc)
         wb_sc_raw = place("wb_sc_raw", [P, PASSES, H // 4], I32, at_wb_sc_raw)
         wo_sc = held("wo_sc", [P, N // 4], I32)
         v_sc_low = held("v_sc_low", [P, PASSES - 1, S // 4], I32)
         gain4 = held("gain4", [P, PACK], F32)
-
-        nc.vector.memset(tab_sc[:], 0)
-        nc.vector.memset(wb_sc_raw[:], 0)
         warm_in = held("warm_in", [P, 8], F32)
         warm_out = held("warm_out", [P, 8], F32)
+
+        nc.gpsimd.memset(tab_sc[:], 0)
+        nc.vector.memset(wb_sc_raw[:], 0)
         nc.vector.memset(warm_in[:], 0.0)
+        nc.vector.memset(wo_sc[:], 0)
         nc.vector.memset(v_sc_low[:], 0)
 
-        def load_tab(a, at):
-            tab[a] = place(f"tab{a}", [P, T], I32, at)
+        tab, wa_raw, g_tab = {}, {}, {}
+
+        def load_tab(a):
+            tab[a] = place(f"tab{a}", [P, T], I32, at_tab[a])
             nc.sync.dma_start(tab[a][:], tab_words[a].rearrange("p n i -> p (n i)").bitcast(I32))
 
-        def load_wa(a, at):
+        def load_wa(a):
             rows = wa[a * P * PACK : (a + 1) * P * PACK, :]
-            wa_raw[a] = place(f"wa_raw{a}", [P, PACK, H], F32, at)
+            wa_raw[a] = place(f"wa_raw{a}", [P, PACK, H], F32, at_wa[a])
             nc.sync.dma_start(wa_raw[a][:], rows.rearrange("(p j) c -> p j c", j=PACK))
 
         g_planes = gT.rearrange("(p t) n -> p t n", t=PACK)
 
-        def load_g(t, at):
-            g_tab[t] = place(f"g_tab{t}", [P, T], F32, at)
+        def load_g(t):
+            g_tab[t] = place(f"g_tab{t}", [P, T], F32, at_g[t])
             nc.sync.dma_start(g_tab[t][:], g_planes[:, t, :])
 
         nc.sync.dma_start(offsets[:], offs)
-        wb_raw = place("wb_raw", [P, PASSES, H // 2], I32, at_wb)
+        wb_raw = place("wb_raw", [P, PASSES, H // 2], I32, at_wb_raw)
         nc.sync.dma_start(wb_raw[:], wb_words.rearrange("a p c -> p a c").bitcast(I32))
-        load_tab(0, at_tab0)
-        load_tab(1, at_tab1)
+        load_tab(0)
+        load_tab(1)
         for q in range(QUADS):
-            (nc.scalar, nc.sync)[q % 2].dma_start(
+            nc.gpsimd.dma_start(
                 tab_sc[32 * q : 32 * q + 4 * PASSES, :],
                 tab_scales[:, 4 * q : 4 * q + 4, :].bitcast(I32),
             )
         for q in range(QUADS):
-            nc.gpsimd.dma_start(
+            nc.scalar.dma_start(
                 wb_sc_raw[32 * q : 32 * q + 4, :, :],
                 wb_scales[:, 4 * q : 4 * q + 4, :].rearrange("a r c -> r a c").bitcast(I32),
             )
-        nc.gpsimd.dma_start(gain4[:], gain.rearrange("(p t) -> p t", t=PACK))
-        nc.vector.memset(wo_sc[:], 0)
+        nc.scalar.dma_start(gain4[:], gain.rearrange("(p t) -> p t", t=PACK))
         for q in range(QUADS):
             nc.gpsimd.dma_start(
                 wo_sc[32 * q : 32 * q + 4, :], wo_scales[0, 4 * q : 4 * q + 4, :].bitcast(I32)
             )
-        load_tab(2, at_tab2)
-        load_wa(0, at_wa0)
 
         nc.scalar.activation(warm_out[:], warm_in[:], ACT.Sigmoid)
 
-        v_codes = [
-            held("v_codes0", [P, S], U32),
-            place("v_codes1", [P, S], U32, at_codes1),
-            place("v_codes2", [P, S], U32, at_codes2),
-        ]
-        v_sc = place("v_sc", [P, S], U8, at_tab0)
-        wa_codes = [held(f"wa_codes{a}", [P, H], U32) for a in range(PASSES)]
-        wa_sc = [held(f"wa_sc{a}", [P, H], U8) for a in range(PASSES)]
         wb_codes = held("wb_codes", [P, PASSES * H // 2], I32)
-        wb_sc = place("wb_sc", [P, PASSES * H], U8, at_wb_sc)
-
-        def gather_words(a):
-            nc.vector.tensor_copy(v_codes[a][:], tab[a][:].bitcast(U32).indirect(offsets[:]))
-
-        def quantize_wa(a):
-            grouped = place(f"grouped{a}", [P, H * PACK], BF16, at_cast[a])
-            for t0 in range(0, PACK, 2):
-                nc.scalar.copy(
-                    grouped[:].rearrange("p (t m j) -> p m j t", t=PACK, j=PACK)[:, :, :, t0 : t0 + 2],
-                    wa_raw[a][:].rearrange("p j (m t) -> p m j t", t=PACK)[:, :, :, t0 : t0 + 2],
-                )
-            nc.vector.quantize_mx(out=wa_codes[a][:].bitcast(FP8X4), scales=wa_sc[a][:], in_=grouped[:])
-
         nc.vector.tensor_copy(
             wb_codes[:].bitcast(U16).rearrange("p (t c i) -> p c t i", t=PACK, i=8),
             wb_raw[:].bitcast(U16).rearrange("p a (c i t) -> p (a c) t i", t=PACK, i=8),
         )
+        wb_sc = place("wb_sc", [P, PASSES * H], U8, at_wb_sc)
+        nc.vector.tensor_copy(
+            wb_sc[:].rearrange("p (t c i) -> p c t i", t=PACK, i=16),
+            wb_sc_raw[:].bitcast(U8).rearrange("p a (c i t) -> p (a c) t i", t=PACK, i=16),
+        )
+        load_tab(2)
+        for a in range(PASSES):
+            load_wa(a)
+
+        v_codes = {}
+
+        def gather_words(a):
+            whole = held(f"v_codes{a}", [P, S], U32)
+            nc.vector.tensor_copy(whole[:], tab[a][:].bitcast(U32).indirect(offsets[:]))
+            for h in range(HALVES):
+                v_codes[a, h] = whole[:, h * HALF : (h + 1) * HALF]
+
+        def entries(j0, width):
+            return offsets[:, j0 // LIST_ROWS : (j0 + width) // LIST_ROWS]
+
         gather_words(0)
+        v_sc = place("v_sc", [P, S], U8, at_v_sc)
         nc.vector.tensor_copy(v_sc[:], tab_sc[:].bitcast(U8).indirect(offsets[:]))
         for a in range(1, PASSES):
             nc.scalar.dma_start(
                 v_sc_low[0:SHIFT_ROWS, a - 1, :], v_sc[4 * a : 4 * a + SHIFT_ROWS, :].bitcast(I32)
             )
-        load_wa(1, at_g0)
+        load_g(0)
+        load_g(1)
         gather_words(1)
-        load_wa(2, at_wa1)
-        nc.vector.tensor_copy(
-            wb_sc[:].rearrange("p (t c i) -> p c t i", t=PACK, i=16),
-            wb_sc_raw[:].bitcast(U8).rearrange("p a (c i t) -> p (a c) t i", t=PACK, i=16),
-        )
-        load_g(0, at_wa2)
-        gather_words(2)
-        load_g(1, at_tab2)
-        quantize_wa(0)
-        load_g(2, at_wa0)
-        load_g(3, at_cast[0])
-        quantize_wa(1)
-        quantize_wa(2)
-        wo_codes = place("wo_codes", [P, N], I32, at_g0)
+        load_g(2)
+        load_g(3)
+        for h in range(HALVES):
+            part = place(f"v_codes2_{h}", [P, HALF], U32, at_codes2[h])
+            nc.vector.tensor_copy(part[:], tab[2][:].bitcast(U32).indirect(entries(h * HALF, HALF)))
+            v_codes[2, h] = part[:]
+        wo_codes = place("wo_codes", [P, N], I32, at_wo)
         nc.sync.dma_start(wo_codes[:], wo_words[0].rearrange("p c i -> p (c i)").bitcast(I32))
 
-        content = [held(f"content{h}", [P, PACK, HALF], F32) for h in range(HALVES)]
-        gate = [place("gate0", [P, PACK, HALF], F32, at_wa1), held("gate1", [P, PACK, HALF], F32)]
-        state = [held(f"state{h}", [P, PACK, HALF], F32) for h in range(HALVES)]
+        wa_codes = [held("wa_codes0", [P, H], U32), held("wa_codes1", [P, H], U32),
+                    place("wa_codes2", [P, H], U32, at_wa_codes2)]
+        wa_sc = [held(f"wa_sc{a}", [P, H], U8) for a in range(PASSES)]
+
+        def quantize_wa(a, copy):
+            grouped = held(f"grouped{a}", [P, H * PACK], BF16)
+            for t0 in range(0, PACK, 2):
+                copy(
+                    grouped[:].rearrange("p (t m j) -> p m j t", t=PACK, j=PACK)[:, :, :, t0 : t0 + 2],
+                    wa_raw[a][:].rearrange("p j (m t) -> p m j t", t=PACK)[:, :, :, t0 : t0 + 2],
+                )
+            nc.vector.quantize_mx(out=wa_codes[a][:].bitcast(FP8X4), scales=wa_sc[a][:], in_=grouped[:])
+
+        quantize_wa(0, nc.scalar.copy)
+        quantize_wa(1, nc.scalar.copy)
+        quantize_wa(2, nc.vector.tensor_copy)
+
+        gate = place("gate", [P, HALVES * PACK, HALF], F32, at_gate)
+        content = held("content", [P, HALVES * PACK, HALF], F32)
         gain_wide = held("gain_wide", [P, HALF // 2], F32)
         nc.scalar.copy(gain_wide[:], gain4[:, PACK - 1 :].to_broadcast([P, HALF // 2]))
 
-        def first_stage(h):
-            cols = slice(h * HALF, (h + 1) * HALF)
-            b_banks = [psum.tile([P, HALF], F32, name="bank") for t in range(PACK)]
-            a_banks = [psum.tile([P, HALF], F32, name="bank") for t in range(PACK)]
-            for a in range(PASSES):
+        b_banks = [psum.tile([P, HALF], F32, name="bank") for u in range(HALVES * PACK)]
+        for a in range(PASSES):
+            for h in range(HALVES):
+                cols = slice(h * HALF, (h + 1) * HALF)
                 low = v_sc[:, cols] if a == 0 else v_sc_low[:, a - 1, :].bitcast(U8)[:, cols]
                 for t in range(PACK):
                     m0 = P * (PASSES * t + a)
                     nc.tensor.matmul_mx(
-                        out=b_banks[t][:],
+                        out=b_banks[PACK * h + t][:],
                         lhsT=wb_codes[:].bitcast(U8)[:, 2 * m0 : 2 * (m0 + P)].bitcast(FP4X4),
                         lhsT_scale=wb_sc[:, m0 : m0 + P],
-                        rhs=v_codes[a][:, cols].bitcast(FP8X4),
+                        rhs=v_codes[a, h].bitcast(FP8X4),
                         rhs_scale=low,
                         start=(a == 0),
                         stop=(a == PASSES - 1),
                     )
+        for u in range(HALVES * PACK):
+            nc.scalar.activation(gate[:, u, :], b_banks[u][:], ACT.Sigmoid)
+        for h in range(HALVES):
+            cols = slice(h * HALF, (h + 1) * HALF)
+            a_banks = [psum.tile([P, HALF], F32, name="bank") for t in range(PACK)]
+            for a in range(PASSES):
                 for t in range(PACK):
                     nc.tensor.matmul_mx(
                         out=a_banks[t][:],
                         lhsT=wa_codes[a][:, P * t : P * (t + 1)].bitcast(FP8X4),
                         lhsT_scale=wa_sc[a][:, P * t : P * (t + 1)],
-                        rhs=v_codes[a][:, cols].bitcast(FP8X4),
+                        rhs=v_codes[a, h].bitcast(FP8X4),
                         rhs_scale=v_sc[4 * a :, cols],
                         start=(a == 0),
                         stop=(a == PASSES - 1),
                     )
             for t in range(PACK):
-                nc.scalar.activation(gate[h][:, t, :], b_banks[t][:], ACT.Sigmoid)
-            for t in range(PACK):
-                nc.scalar.activation(content[h][:, t, :], a_banks[t][:], ACT.Tanh)
+                nc.scalar.activation(content[:, PACK * h + t, :], a_banks[t][:], ACT.Tanh)
+
+        state = [place(f"state{h}", [P, PACK, HALF], F32, at_state[h]) for h in range(HALVES)]
+        picked = [held(f"picked{t}", [P, S], F32) for t in range(PACK - 1)]
+        for t in range(PACK - 1):
+            nc.vector.tensor_copy(picked[t][:], g_tab[t][:].indirect(offsets[:]))
+        for h in range(HALVES):
+            for t in range(PACK - 1):
+                nc.scalar.activation(
+                    state[h][:, t, :], picked[t][:, h * HALF : (h + 1) * HALF], ACT.Copy, scale=gain4[:, t : t + 1]
+                )
 
         out_rows = out.rearrange("(c p) j -> p c j", p=P)
 
-        def gather_state(t, j0, width):
-            h, c0 = divmod(j0, HALF)
-            nc.vector.tensor_tensor(
-                state[h][:, t, c0 : c0 + width],
-                g_tab[t][:].indirect(offsets[:, j0 // LIST_ROWS : (j0 + width) // LIST_ROWS]),
-                gain_wide[:, :width],
-                ALU.mult,
-            )
-
         def gate_content(j0, width):
             h, c0 = divmod(j0, HALF)
-            cols = slice(c0, c0 + width)
-            gated = held("gated", [P, PACK, width], F32)
+            gated = place(f"gated{j0}", [P, PACK, width], F32, at_g[2] + (j0 // width % 2) * PACK * width * 4)
             for t in range(PACK):
                 nc.vector.scalar_tensor_tensor(
-                    gated[:, t, :], content[h][:, t, cols], gain4[:, t : t + 1], gate[h][:, t, cols],
-                    ALU.mult, ALU.mult,
+                    gated[:, t, :], content[:, PACK * h + t, c0 : c0 + width], gain4[:, t : t + 1],
+                    gate[:, PACK * h + t, c0 : c0 + width], ALU.mult, ALU.mult,
                 )
             return gated
 
-        def quantize_h(gated, g0, j0, width):
+        def gather_last_state(j0, width):
             h, c0 = divmod(j0, HALF)
-            cols = slice(c0, c0 + width)
+            nc.vector.tensor_tensor(
+                state[h][:, PACK - 1, c0 : c0 + width], g_tab[PACK - 1][:].indirect(entries(j0, width)),
+                gain_wide[:, :width], ALU.mult,
+            )
+
+        def sum_h(gated, g0, j0, width):
+            h, c0 = divmod(j0, HALF)
             h_grouped = ring2.tile([P, width * PACK], BF16, name="h_grouped", align_bytes=64)
             nc.vector.tensor_tensor(
                 h_grouped[:].rearrange("p (c i t) -> p c t i", i=2, t=PACK),
                 gated[:, :, j0 - g0 : j0 - g0 + width].rearrange("p t (c i) -> p c t i", i=2),
-                state[h][:, :, cols].rearrange("p t (c i) -> p c t i", i=2),
+                state[h][:, :, c0 : c0 + width].rearrange("p t (c i) -> p c t i", i=2),
                 ALU.add,
             )
+            return h_grouped
+
+        def project(h_grouped, j0, width):
             h_codes = ring2.tile([P, width], U32, name="h_codes", align_bytes=64)
             h_sc = ring2.tile([P, width], U8, name="h_sc", align_bytes=64)
             nc.vector.quantize_mx(out=h_codes[:].bitcast(FP8X4), scales=h_sc[:], in_=h_grouped[:])
-            return h_codes, h_sc
-
-        def project(j0, width, h_codes, h_sc, share_copies):
             staged = ring3.tile([P, CHUNKS, width], F32, name="staged")
             per_bank = min(HALF // width, CHUNKS // 2)
             for c0 in range(0, CHUNKS, per_bank):
@@ -252,29 +272,22 @@ def tile_list_gated_neighbor_messages_kernel(
                         start=True,
                         stop=True,
                     )
-                if share_copies and c0 > 0:
+                if j0 + width == S and c0 > 0:
                     nc.vector.tensor_copy(staged[:, chunks, :], bank[:])
                 else:
                     nc.scalar.copy(staged[:, chunks, :], bank[:])
                 nc.sync.dma_start(out_rows[:, chunks, j0 : j0 + width], staged[:, chunks, :])
 
-        def second_stage(j0, widths):
-            total = sum(widths)
-            gated = gate_content(j0, total)
-            gather_state(PACK - 1, j0, total)
-            starts = [j0 + sum(widths[:i]) for i in range(len(widths))]
-            operands = [quantize_h(gated, j0, start, width) for start, width in zip(starts, widths)]
-            for start, width, (h_codes, h_sc) in zip(starts, widths, operands):
-                project(start, width, h_codes, h_sc, share_copies=(j0 + total == S))
-
-        for h in range(HALVES):
-            first_stage(h)
-        for t in range(PACK - 1):
-            picked = held(f"picked{t}", [P, S], F32)
-            nc.vector.tensor_copy(picked[:], g_tab[t][:].indirect(offsets[:]))
-            for h in range(HALVES):
-                nc.scalar.activation(
-                    state[h][:, t, :], picked[:, h * HALF : (h + 1) * HALF], ACT.Copy, scale=gain4[:, t : t + 1]
-                )
-        for group in GROUPS:
-            second_stage(*group)
+        GROUP = HALF // 2
+        gated = {g0: gate_content(g0, GROUP) for g0 in (0, GROUP)}
+        gather_last_state(0, GROUP)
+        j0 = 0
+        for width in PIECES:
+            g0 = j0 - j0 % GROUP
+            h_grouped = sum_h(gated[g0], g0, j0, width)
+            if j0 == g0 and g0 + GROUP < S:
+                gather_last_state(g0 + GROUP, GROUP)
+            project(h_grouped, j0, width)
+            if j0 + width == g0 + GROUP and g0 + 2 * GROUP < S:
+                gated[g0 + 2 * GROUP] = gate_content(g0 + 2 * GROUP, GROUP)
+            j0 += width

@@ -28,6 +28,24 @@ SHIFT_ROWS = 112
 PIECES = (256, 256, 256, 128, 128)
 KIB = 1024
 LAP = 64
+ROWS = (
+    (("v_codes1", 4 * KIB), ("wb_sc_raw", 1536), ("wa_raw2", 8 * KIB)),
+    (("g_tab3", 8 * KIB), ("wa_raw0", 8 * KIB), ("tab0", 8 * KIB), ("wa_raw1", 8 * KIB), ("gate", 16 * KIB)),
+    (("g_tab0", 8 * KIB), ("tab1", 8 * KIB), ("g_tab1", 8 * KIB)),
+    (("tab2", 8 * KIB), ("g_tab2", 8 * KIB)),
+    (("tab_sc", 2 * KIB), ("wb_sc", 1536)),
+    (("state0", 8 * KIB), ("wa_codes2", 2 * KIB), ("state1", 8 * KIB)),
+)
+INSIDE = {
+    "v_codes2_0": ("tab1", KIB),
+    "v_codes2_1": ("tab1", 3 * KIB),
+    "v_sc": ("tab0", KIB),
+    "wo_codes": ("wa_raw1", KIB),
+    "gated0": ("g_tab2", 0),
+    "gated256": ("g_tab2", 4 * KIB),
+    "gated512": ("g_tab2", 0),
+    "gated768": ("g_tab2", 4 * KIB),
+}
 
 
 def tile_list_gated_neighbor_messages_kernel(
@@ -46,25 +64,26 @@ def tile_list_gated_neighbor_messages_kernel(
         def held(name, shape, dtype):
             return keep.tile(shape, dtype, name=name, align_bytes=64)
 
-        def place(name, shape, dtype, at):
-            return placed.tile(shape, dtype, name=name, align_bytes=64, offset=at)
+        at, free = {}, 0
+        for row in ROWS:
+            for name, size in row:
+                at[name] = free
+                free = free + size - LAP
+            free = free + LAP
+        for name, (host, shift) in INSIDE.items():
+            at[name] = at[host] + shift
 
-        at_tab = (62 * KIB - LAP, 87 * KIB - LAP, 0)
-        at_wa = (11 * KIB - 2 * LAP, 36 * KIB, 45 * KIB + 512 - 2 * LAP)
-        at_g = (54 * KIB, 70 * KIB - 2 * LAP, 79 * KIB, 95 * KIB - 2 * LAP)
-        at_wb_raw, at_wb_sc, at_wb_sc_raw = 8 * KIB - LAP, 8 * KIB + LAP, 44 * KIB - LAP
-        at_gate, at_v_sc, at_wo = 19 * KIB - 3 * LAP, 63 * KIB, 0
-        at_tab_sc, at_codes2 = 104 * KIB, (103 * KIB + 512, 105 * KIB + 512)
-        at_state, at_wa_codes2 = (108 * KIB, 118 * KIB - 2 * LAP), 116 * KIB - LAP
+        def place(name, shape, dtype):
+            return placed.tile(shape, dtype, name=name, align_bytes=64, offset=at[name])
 
-        tab_sc = place("tab_sc", [P, T // 4], I32, at_tab_sc)
-        wb_sc_raw = place("wb_sc_raw", [P, PASSES, H // 4], I32, at_wb_sc_raw)
+        tab_sc = place("tab_sc", [P, T // 4], I32)
         wo_sc = held("wo_sc", [P, N // 4], I32)
         v_sc_low = held("v_sc_low", [P, PASSES - 1, S // 4], I32)
         gain4 = held("gain4", [P, PACK], F32)
         warm_in = held("warm_in", [P, 8], F32)
         warm_out = held("warm_out", [P, 8], F32)
 
+        wb_sc_raw = place("wb_sc_raw", [P, PASSES, H // 4], I32)
         nc.gpsimd.memset(tab_sc[:], 0)
         nc.vector.memset(wb_sc_raw[:], 0)
         nc.vector.memset(warm_in[:], 0.0)
@@ -74,36 +93,39 @@ def tile_list_gated_neighbor_messages_kernel(
         tab, wa_raw, g_tab = {}, {}, {}
 
         def load_tab(a):
-            tab[a] = place(f"tab{a}", [P, T], I32, at_tab[a])
+            tab[a] = place(f"tab{a}", [P, T], I32)
             nc.sync.dma_start(tab[a][:], tab_words[a].rearrange("p n i -> p (n i)").bitcast(I32))
 
         def load_wa(a):
             rows = wa[a * P * PACK : (a + 1) * P * PACK, :]
-            wa_raw[a] = place(f"wa_raw{a}", [P, PACK, H], F32, at_wa[a])
+            wa_raw[a] = place(f"wa_raw{a}", [P, PACK, H], F32)
             nc.sync.dma_start(wa_raw[a][:], rows.rearrange("(p j) c -> p j c", j=PACK))
 
         g_planes = gT.rearrange("(p t) n -> p t n", t=PACK)
 
         def load_g(t):
-            g_tab[t] = place(f"g_tab{t}", [P, T], F32, at_g[t])
+            g_tab[t] = place(f"g_tab{t}", [P, T], F32)
             nc.sync.dma_start(g_tab[t][:], g_planes[:, t, :])
 
+        def load_tab_scales(q, queue):
+            queue.dma_start(
+                tab_sc[32 * q : 32 * q + 4 * PASSES, :], tab_scales[:, 4 * q : 4 * q + 4, :].bitcast(I32)
+            )
+
         nc.sync.dma_start(offsets[:], offs)
-        wb_raw = place("wb_raw", [P, PASSES, H // 2], I32, at_wb_raw)
+        wb_raw = held("wb_raw", [P, PASSES, H // 2], I32)
         nc.sync.dma_start(wb_raw[:], wb_words.rearrange("a p c -> p a c").bitcast(I32))
         load_tab(0)
+        for q in range(QUADS):
+            load_tab_scales(q, (nc.sync, nc.scalar)[q // 2])
         load_tab(1)
         for q in range(QUADS):
-            nc.gpsimd.dma_start(
-                tab_sc[32 * q : 32 * q + 4 * PASSES, :],
-                tab_scales[:, 4 * q : 4 * q + 4, :].bitcast(I32),
-            )
-        for q in range(QUADS):
-            nc.scalar.dma_start(
+            nc.sync.dma_start(
                 wb_sc_raw[32 * q : 32 * q + 4, :, :],
                 wb_scales[:, 4 * q : 4 * q + 4, :].rearrange("a r c -> r a c").bitcast(I32),
             )
-        nc.scalar.dma_start(gain4[:], gain.rearrange("(p t) -> p t", t=PACK))
+        load_tab(2)
+        nc.gpsimd.dma_start(gain4[:], gain.rearrange("(p t) -> p t", t=PACK))
         for q in range(QUADS):
             nc.gpsimd.dma_start(
                 wo_sc[32 * q : 32 * q + 4, :], wo_scales[0, 4 * q : 4 * q + 4, :].bitcast(I32)
@@ -116,19 +138,10 @@ def tile_list_gated_neighbor_messages_kernel(
             wb_codes[:].bitcast(U16).rearrange("p (t c i) -> p c t i", t=PACK, i=8),
             wb_raw[:].bitcast(U16).rearrange("p a (c i t) -> p (a c) t i", t=PACK, i=8),
         )
-        wb_sc = place("wb_sc", [P, PASSES * H], U8, at_wb_sc)
-        nc.vector.tensor_copy(
-            wb_sc[:].rearrange("p (t c i) -> p c t i", t=PACK, i=16),
-            wb_sc_raw[:].bitcast(U8).rearrange("p a (c i t) -> p (a c) t i", t=PACK, i=16),
-        )
-        load_tab(2)
-        for a in range(PASSES):
-            load_wa(a)
 
         v_codes = {}
 
-        def gather_words(a):
-            whole = held(f"v_codes{a}", [P, S], U32)
+        def gather_words(a, whole):
             nc.vector.tensor_copy(whole[:], tab[a][:].bitcast(U32).indirect(offsets[:]))
             for h in range(HALVES):
                 v_codes[a, h] = whole[:, h * HALF : (h + 1) * HALF]
@@ -136,27 +149,32 @@ def tile_list_gated_neighbor_messages_kernel(
         def entries(j0, width):
             return offsets[:, j0 // LIST_ROWS : (j0 + width) // LIST_ROWS]
 
-        gather_words(0)
-        v_sc = place("v_sc", [P, S], U8, at_v_sc)
+        gather_words(0, held("v_codes0", [P, S], U32))
+        load_wa(0)
+        load_wa(1)
+        v_sc = place("v_sc", [P, S], U8)
         nc.vector.tensor_copy(v_sc[:], tab_sc[:].bitcast(U8).indirect(offsets[:]))
         for a in range(1, PASSES):
             nc.scalar.dma_start(
                 v_sc_low[0:SHIFT_ROWS, a - 1, :], v_sc[4 * a : 4 * a + SHIFT_ROWS, :].bitcast(I32)
             )
+        wb_sc = place("wb_sc", [P, PASSES * H], U8)
+        nc.vector.tensor_copy(
+            wb_sc[:].rearrange("p (t c i) -> p c t i", t=PACK, i=16),
+            wb_sc_raw[:].bitcast(U8).rearrange("p a (c i t) -> p (a c) t i", t=PACK, i=16),
+        )
+        load_wa(2)
+        gather_words(1, place("v_codes1", [P, S], U32))
         load_g(0)
         load_g(1)
-        gather_words(1)
-        load_g(2)
-        load_g(3)
         for h in range(HALVES):
-            part = place(f"v_codes2_{h}", [P, HALF], U32, at_codes2[h])
+            part = place(f"v_codes2_{h}", [P, HALF], U32)
             nc.vector.tensor_copy(part[:], tab[2][:].bitcast(U32).indirect(entries(h * HALF, HALF)))
             v_codes[2, h] = part[:]
-        wo_codes = place("wo_codes", [P, N], I32, at_wo)
-        nc.sync.dma_start(wo_codes[:], wo_words[0].rearrange("p c i -> p (c i)").bitcast(I32))
+        load_g(2)
 
         wa_codes = [held("wa_codes0", [P, H], U32), held("wa_codes1", [P, H], U32),
-                    place("wa_codes2", [P, H], U32, at_wa_codes2)]
+                    place("wa_codes2", [P, H], U32)]
         wa_sc = [held(f"wa_sc{a}", [P, H], U8) for a in range(PASSES)]
 
         def quantize_wa(a, copy):
@@ -169,10 +187,13 @@ def tile_list_gated_neighbor_messages_kernel(
             nc.vector.quantize_mx(out=wa_codes[a][:].bitcast(FP8X4), scales=wa_sc[a][:], in_=grouped[:])
 
         quantize_wa(0, nc.scalar.copy)
+        load_g(3)
         quantize_wa(1, nc.scalar.copy)
+        wo_codes = place("wo_codes", [P, N], I32)
+        nc.sync.dma_start(wo_codes[:], wo_words[0].rearrange("p c i -> p (c i)").bitcast(I32))
         quantize_wa(2, nc.vector.tensor_copy)
 
-        gate = place("gate", [P, HALVES * PACK, HALF], F32, at_gate)
+        gate = place("gate", [P, HALVES * PACK, HALF], F32)
         content = held("content", [P, HALVES * PACK, HALF], F32)
         gain_wide = held("gain_wide", [P, HALF // 2], F32)
         nc.scalar.copy(gain_wide[:], gain4[:, PACK - 1 :].to_broadcast([P, HALF // 2]))
@@ -212,7 +233,7 @@ def tile_list_gated_neighbor_messages_kernel(
             for t in range(PACK):
                 nc.scalar.activation(content[:, PACK * h + t, :], a_banks[t][:], ACT.Tanh)
 
-        state = [place(f"state{h}", [P, PACK, HALF], F32, at_state[h]) for h in range(HALVES)]
+        state = [place(f"state{h}", [P, PACK, HALF], F32) for h in range(HALVES)]
         picked = [held(f"picked{t}", [P, S], F32) for t in range(PACK - 1)]
         for t in range(PACK - 1):
             nc.vector.tensor_copy(picked[t][:], g_tab[t][:].indirect(offsets[:]))
@@ -226,7 +247,7 @@ def tile_list_gated_neighbor_messages_kernel(
 
         def gate_content(j0, width):
             h, c0 = divmod(j0, HALF)
-            gated = place(f"gated{j0}", [P, PACK, width], F32, at_g[2] + (j0 // width % 2) * PACK * width * 4)
+            gated = place(f"gated{j0}", [P, PACK, width], F32)
             for t in range(PACK):
                 nc.vector.scalar_tensor_tensor(
                     gated[:, t, :], content[:, PACK * h + t, c0 : c0 + width], gain4[:, t : t + 1],

@@ -30,21 +30,24 @@ KIB = 1024
 LAP = 64
 ROWS = (
     (("v_codes1", 4 * KIB), ("wb_sc_raw", 1536), ("wa_raw2", 8 * KIB)),
-    (("g_tab3", 8 * KIB), ("wa_raw0", 8 * KIB), ("tab0", 8 * KIB), ("wa_raw1", 8 * KIB), ("gate", 16 * KIB)),
+    (("v_sc", KIB), ("tab0", 8 * KIB), ("tab2", 8 * KIB), ("g_tab3", 8 * KIB)),
     (("g_tab0", 8 * KIB), ("tab1", 8 * KIB), ("g_tab1", 8 * KIB)),
-    (("tab2", 8 * KIB), ("g_tab2", 8 * KIB)),
+    (("wa_raw0", 8 * KIB),),
     (("tab_sc", 2 * KIB), ("wb_sc", 1536)),
-    (("state0", 8 * KIB), ("wa_codes2", 2 * KIB), ("state1", 8 * KIB)),
+    (("state0", 8 * KIB), ("wb_codes", 3 * KIB)),
+    (("wa_codes2", 2 * KIB), ("state1", 8 * KIB)),
+    (("grouped2", 4 * KIB), ("gained", 8 * KIB)),
+    (("picked2_0", 2 * KIB), ("content1", 8 * KIB)),
+    (("wa_raw1", 8 * KIB), ("gate", 16 * KIB)),
+    (("gated0", 4 * KIB),),
+    (("gated256", 4 * KIB),),
 )
 INSIDE = {
-    "v_codes2_0": ("tab1", KIB),
-    "v_codes2_1": ("tab1", 3 * KIB),
-    "v_sc": ("tab0", KIB),
-    "wo_codes": ("wa_raw1", KIB),
-    "gated0": ("g_tab2", 0),
-    "gated256": ("g_tab2", 4 * KIB),
-    "gated512": ("g_tab2", 0),
-    "gated768": ("g_tab2", 4 * KIB),
+    "g_tab2": ("tab0", LAP),
+    "wa_codes1": ("tab2", KIB),
+    "wo_codes": ("wa_raw2", 2 * KIB),
+    "gated512": ("gated0", 0),
+    "gated768": ("gated256", 0),
 }
 
 
@@ -124,7 +127,8 @@ def tile_list_gated_neighbor_messages_kernel(
                 wb_sc_raw[32 * q : 32 * q + 4, :, :],
                 wb_scales[:, 4 * q : 4 * q + 4, :].rearrange("a r c -> r a c").bitcast(I32),
             )
-        load_tab(2)
+        load_wa(0)
+        load_wa(1)
         nc.gpsimd.dma_start(gain4[:], gain.rearrange("(p t) -> p t", t=PACK))
         for q in range(QUADS):
             nc.gpsimd.dma_start(
@@ -133,7 +137,7 @@ def tile_list_gated_neighbor_messages_kernel(
 
         nc.scalar.activation(warm_out[:], warm_in[:], ACT.Sigmoid)
 
-        wb_codes = held("wb_codes", [P, PASSES * H // 2], I32)
+        wb_codes = place("wb_codes", [P, PASSES * H // 2], I32)
         nc.vector.tensor_copy(
             wb_codes[:].bitcast(U16).rearrange("p (t c i) -> p c t i", t=PACK, i=8),
             wb_raw[:].bitcast(U16).rearrange("p a (c i t) -> p (a c) t i", t=PACK, i=8),
@@ -150,8 +154,7 @@ def tile_list_gated_neighbor_messages_kernel(
             return offsets[:, j0 // LIST_ROWS : (j0 + width) // LIST_ROWS]
 
         gather_words(0, held("v_codes0", [P, S], U32))
-        load_wa(0)
-        load_wa(1)
+        load_tab(2)
         v_sc = place("v_sc", [P, S], U8)
         nc.vector.tensor_copy(v_sc[:], tab_sc[:].bitcast(U8).indirect(offsets[:]))
         for a in range(1, PASSES):
@@ -168,17 +171,18 @@ def tile_list_gated_neighbor_messages_kernel(
         load_g(0)
         load_g(1)
         for h in range(HALVES):
-            part = place(f"v_codes2_{h}", [P, HALF], U32)
+            part = held(f"v_codes2_{h}", [P, HALF], U32)
             nc.vector.tensor_copy(part[:], tab[2][:].bitcast(U32).indirect(entries(h * HALF, HALF)))
             v_codes[2, h] = part[:]
         load_g(2)
+        load_g(3)
 
-        wa_codes = [held("wa_codes0", [P, H], U32), held("wa_codes1", [P, H], U32),
+        wa_codes = [held("wa_codes0", [P, H], U32), place("wa_codes1", [P, H], U32),
                     place("wa_codes2", [P, H], U32)]
         wa_sc = [held(f"wa_sc{a}", [P, H], U8) for a in range(PASSES)]
 
         def quantize_wa(a, copy):
-            grouped = held(f"grouped{a}", [P, H * PACK], BF16)
+            grouped = (held, held, place)[a](f"grouped{a}", [P, H * PACK], BF16)
             for t0 in range(0, PACK, 2):
                 copy(
                     grouped[:].rearrange("p (t m j) -> p m j t", t=PACK, j=PACK)[:, :, :, t0 : t0 + 2],
@@ -187,72 +191,111 @@ def tile_list_gated_neighbor_messages_kernel(
             nc.vector.quantize_mx(out=wa_codes[a][:].bitcast(FP8X4), scales=wa_sc[a][:], in_=grouped[:])
 
         quantize_wa(0, nc.scalar.copy)
-        load_g(3)
         quantize_wa(1, nc.scalar.copy)
+        quantize_wa(2, nc.vector.tensor_copy)
         wo_codes = place("wo_codes", [P, N], I32)
         nc.sync.dma_start(wo_codes[:], wo_words[0].rearrange("p c i -> p (c i)").bitcast(I32))
-        quantize_wa(2, nc.vector.tensor_copy)
 
         gate = place("gate", [P, HALVES * PACK, HALF], F32)
-        content = held("content", [P, HALVES * PACK, HALF], F32)
         gain_wide = held("gain_wide", [P, HALF // 2], F32)
         nc.scalar.copy(gain_wide[:], gain4[:, PACK - 1 :].to_broadcast([P, HALF // 2]))
 
-        b_banks = [psum.tile([P, HALF], F32, name="bank") for u in range(HALVES * PACK)]
-        for a in range(PASSES):
-            for h in range(HALVES):
-                cols = slice(h * HALF, (h + 1) * HALF)
-                low = v_sc[:, cols] if a == 0 else v_sc_low[:, a - 1, :].bitcast(U8)[:, cols]
-                for t in range(PACK):
-                    m0 = P * (PASSES * t + a)
-                    nc.tensor.matmul_mx(
-                        out=b_banks[PACK * h + t][:],
-                        lhsT=wb_codes[:].bitcast(U8)[:, 2 * m0 : 2 * (m0 + P)].bitcast(FP4X4),
-                        lhsT_scale=wb_sc[:, m0 : m0 + P],
-                        rhs=v_codes[a, h].bitcast(FP8X4),
-                        rhs_scale=low,
-                        start=(a == 0),
-                        stop=(a == PASSES - 1),
-                    )
-        for u in range(HALVES * PACK):
-            nc.scalar.activation(gate[:, u, :], b_banks[u][:], ACT.Sigmoid)
-        for h in range(HALVES):
-            cols = slice(h * HALF, (h + 1) * HALF)
-            a_banks = [psum.tile([P, HALF], F32, name="bank") for t in range(PACK)]
-            for a in range(PASSES):
-                for t in range(PACK):
-                    nc.tensor.matmul_mx(
-                        out=a_banks[t][:],
-                        lhsT=wa_codes[a][:, P * t : P * (t + 1)].bitcast(FP8X4),
-                        lhsT_scale=wa_sc[a][:, P * t : P * (t + 1)],
-                        rhs=v_codes[a, h].bitcast(FP8X4),
-                        rhs_scale=v_sc[4 * a :, cols],
-                        start=(a == 0),
-                        stop=(a == PASSES - 1),
-                    )
-            for t in range(PACK):
-                nc.scalar.activation(content[:, PACK * h + t, :], a_banks[t][:], ACT.Tanh)
+        banks, content, state, picked = {}, {}, {}, {}
 
-        state = [place(f"state{h}", [P, PACK, HALF], F32) for h in range(HALVES)]
-        picked = [held(f"picked{t}", [P, S], F32) for t in range(PACK - 1)]
-        for t in range(PACK - 1):
-            nc.vector.tensor_copy(picked[t][:], g_tab[t][:].indirect(offsets[:]))
-        for h in range(HALVES):
-            for t in range(PACK - 1):
-                nc.scalar.activation(
-                    state[h][:, t, :], picked[t][:, h * HALF : (h + 1) * HALF], ACT.Copy, scale=gain4[:, t : t + 1]
+        def gate_pass(h, a):
+            cols = slice(h * HALF, (h + 1) * HALF)
+            low = v_sc[:, cols] if a == 0 else v_sc_low[:, a - 1, :].bitcast(U8)[:, cols]
+            for t in range(PACK):
+                m0 = P * (PASSES * t + a)
+                nc.tensor.matmul_mx(
+                    out=banks["gate", h][t][:],
+                    lhsT=wb_codes[:].bitcast(U8)[:, 2 * m0 : 2 * (m0 + P)].bitcast(FP4X4),
+                    lhsT_scale=wb_sc[:, m0 : m0 + P],
+                    rhs=v_codes[a, h].bitcast(FP8X4),
+                    rhs_scale=low,
+                    start=(a == 0),
+                    stop=(a == PASSES - 1),
                 )
+
+        def content_pass(h, a):
+            cols = slice(h * HALF, (h + 1) * HALF)
+            for t in range(PACK):
+                nc.tensor.matmul_mx(
+                    out=banks["content", h][t][:],
+                    lhsT=wa_codes[a][:, P * t : P * (t + 1)].bitcast(FP8X4),
+                    lhsT_scale=wa_sc[a][:, P * t : P * (t + 1)],
+                    rhs=v_codes[a, h].bitcast(FP8X4),
+                    rhs_scale=v_sc[4 * a :, cols],
+                    start=(a == 0),
+                    stop=(a == PASSES - 1),
+                )
+
+        def take_banks(kind, h):
+            banks[kind, h] = [psum.tile([P, HALF], F32, name="bank") for t in range(PACK)]
+
+        def apply_sigmoid(h):
+            for t in range(PACK):
+                nc.scalar.activation(gate[:, PACK * h + t, :], banks["gate", h][t][:], ACT.Sigmoid)
+
+        def apply_tanh(h):
+            content[h] = (held, place)[h](f"content{h}", [P, PACK, HALF], F32)
+            for t in range(PACK):
+                nc.scalar.activation(content[h][:, t, :], banks["content", h][t][:], ACT.Tanh)
+
+        take_banks("gate", 0)
+        take_banks("content", 0)
+        for a in range(PASSES):
+            gate_pass(0, a)
+        for a in range(PASSES):
+            content_pass(0, a)
+        apply_sigmoid(0)
+        gained = place("gained", [P, PACK, HALF], F32)
+        for t in range(PACK):
+            nc.gpsimd.tensor_scalar(gained[:, t, :], gate[:, t, :], gain4[:, t : t + 1], 0.0, ALU.mult, ALU.add)
+        apply_tanh(0)
+        take_banks("gate", 1)
+        for a in range(PASSES):
+            gate_pass(1, a)
+        apply_sigmoid(1)
+        take_banks("content", 1)
+        for a in range(PASSES):
+            content_pass(1, a)
+
+        def scale_state(h):
+            state[h] = place(f"state{h}", [P, PACK, HALF], F32)
+            for t in range(PACK - 1 + h):
+                nc.scalar.activation(state[h][:, t, :], picked[t, h], ACT.Copy, scale=gain4[:, t : t + 1])
+
+        for t in range(PACK - 2):
+            whole = held(f"picked{t}", [P, S], F32)
+            nc.vector.tensor_copy(whole[:], g_tab[t][:].indirect(offsets[:]))
+            for h in range(HALVES):
+                picked[t, h] = whole[:, h * HALF : (h + 1) * HALF]
+        for h in range(HALVES):
+            part = (place, held)[h](f"picked2_{h}", [P, HALF], F32)
+            nc.vector.tensor_copy(part[:], g_tab[2][:].indirect(entries(h * HALF, HALF)))
+            picked[2, h] = part[:]
+        last = held("picked3_1", [P, HALF], F32)
+        nc.vector.tensor_copy(last[:], g_tab[3][:].indirect(entries(HALF, HALF)))
+        picked[3, 1] = last[:]
+        scale_state(0)
+        apply_tanh(1)
+        scale_state(1)
 
         out_rows = out.rearrange("(c p) j -> p c j", p=P)
 
         def gate_content(j0, width):
             h, c0 = divmod(j0, HALF)
+            cols = slice(c0, c0 + width)
             gated = place(f"gated{j0}", [P, PACK, width], F32)
             for t in range(PACK):
-                nc.vector.scalar_tensor_tensor(
-                    gated[:, t, :], content[:, PACK * h + t, c0 : c0 + width], gain4[:, t : t + 1],
-                    gate[:, PACK * h + t, c0 : c0 + width], ALU.mult, ALU.mult,
-                )
+                if h == 0:
+                    nc.gpsimd.tensor_tensor(gated[:, t, :], content[h][:, t, cols], gained[:, t, cols], ALU.mult)
+                else:
+                    nc.vector.scalar_tensor_tensor(
+                        gated[:, t, :], content[h][:, t, cols], gain4[:, t : t + 1],
+                        gate[:, PACK * h + t, cols], ALU.mult, ALU.mult,
+                    )
             return gated
 
         def gather_last_state(j0, width):
@@ -306,7 +349,7 @@ def tile_list_gated_neighbor_messages_kernel(
         for width in PIECES:
             g0 = j0 - j0 % GROUP
             h_grouped = sum_h(gated[g0], g0, j0, width)
-            if j0 == g0 and g0 + GROUP < S:
+            if j0 == g0 and g0 + GROUP < HALF:
                 gather_last_state(g0 + GROUP, GROUP)
             project(h_grouped, j0, width)
             if j0 + width == g0 + GROUP and g0 + 2 * GROUP < S:

@@ -29,23 +29,21 @@ PIECES = (256, 256, 256, 128, 128)
 KIB = 1024
 LAP = 64
 ROWS = (
-    (("v_codes1", 4 * KIB), ("wb_sc_raw", 1536), ("wa_raw2", 8 * KIB)),
-    (("v_sc", KIB), ("tab0", 8 * KIB), ("tab2", 8 * KIB), ("g_tab3", 8 * KIB)),
+    (("v_codes1", 4 * KIB), ("wb_sc_raw", 1536), ("tab2", 8 * KIB)),
+    (("v_sc", KIB), ("tab0", 8 * KIB), ("wa_raw2", 8 * KIB), ("gate", 16 * KIB)),
     (("g_tab0", 8 * KIB), ("tab1", 8 * KIB), ("g_tab1", 8 * KIB)),
-    (("wa_raw0", 8 * KIB),),
+    (("g_tab2", 8 * KIB), ("wa_raw0", 8 * KIB)),
+    (("g_tab3", 8 * KIB), ("wa_raw1", 8 * KIB)),
     (("tab_sc", 2 * KIB), ("wb_sc", 1536)),
     (("state0", 8 * KIB), ("wb_codes", 3 * KIB)),
-    (("wa_codes2", 2 * KIB), ("state1", 8 * KIB)),
-    (("grouped2", 4 * KIB), ("gained", 8 * KIB)),
     (("picked2_0", 2 * KIB), ("content1", 8 * KIB)),
-    (("wa_raw1", 8 * KIB), ("gate", 16 * KIB)),
+    (("gained", 8 * KIB), ("state1", 8 * KIB)),
     (("gated0", 4 * KIB),),
     (("gated256", 4 * KIB),),
 )
 INSIDE = {
-    "g_tab2": ("tab0", LAP),
-    "wa_codes1": ("tab2", KIB),
     "wo_codes": ("wa_raw2", 2 * KIB),
+    "wa_codes2": ("tab2", KIB),
     "gated512": ("gated0", 0),
     "gated768": ("gated256", 0),
 }
@@ -154,11 +152,11 @@ def tile_list_gated_neighbor_messages_kernel(
             return offsets[:, j0 // LIST_ROWS : (j0 + width) // LIST_ROWS]
 
         gather_words(0, held("v_codes0", [P, S], U32))
-        load_tab(2)
+        load_wa(2)
         v_sc = place("v_sc", [P, S], U8)
         nc.vector.tensor_copy(v_sc[:], tab_sc[:].bitcast(U8).indirect(offsets[:]))
         for a in range(1, PASSES):
-            nc.scalar.dma_start(
+            nc.sync.dma_start(
                 v_sc_low[0:SHIFT_ROWS, a - 1, :], v_sc[4 * a : 4 * a + SHIFT_ROWS, :].bitcast(I32)
             )
         wb_sc = place("wb_sc", [P, PASSES * H], U8)
@@ -166,23 +164,17 @@ def tile_list_gated_neighbor_messages_kernel(
             wb_sc[:].rearrange("p (t c i) -> p c t i", t=PACK, i=16),
             wb_sc_raw[:].bitcast(U8).rearrange("p a (c i t) -> p (a c) t i", t=PACK, i=16),
         )
-        load_wa(2)
+        load_tab(2)
         gather_words(1, place("v_codes1", [P, S], U32))
         load_g(0)
         load_g(1)
-        for h in range(HALVES):
-            part = held(f"v_codes2_{h}", [P, HALF], U32)
-            nc.vector.tensor_copy(part[:], tab[2][:].bitcast(U32).indirect(entries(h * HALF, HALF)))
-            v_codes[2, h] = part[:]
-        load_g(2)
-        load_g(3)
 
-        wa_codes = [held("wa_codes0", [P, H], U32), place("wa_codes1", [P, H], U32),
+        wa_codes = [held("wa_codes0", [P, H], U32), held("wa_codes1", [P, H], U32),
                     place("wa_codes2", [P, H], U32)]
         wa_sc = [held(f"wa_sc{a}", [P, H], U8) for a in range(PASSES)]
 
         def quantize_wa(a, copy):
-            grouped = (held, held, place)[a](f"grouped{a}", [P, H * PACK], BF16)
+            grouped = held(f"grouped{a}", [P, H * PACK], BF16)
             for t0 in range(0, PACK, 2):
                 copy(
                     grouped[:].rearrange("p (t m j) -> p m j t", t=PACK, j=PACK)[:, :, :, t0 : t0 + 2],
@@ -191,8 +183,14 @@ def tile_list_gated_neighbor_messages_kernel(
             nc.vector.quantize_mx(out=wa_codes[a][:].bitcast(FP8X4), scales=wa_sc[a][:], in_=grouped[:])
 
         quantize_wa(0, nc.scalar.copy)
+        load_g(2)
         quantize_wa(1, nc.scalar.copy)
-        quantize_wa(2, nc.vector.tensor_copy)
+        load_g(3)
+        for h in range(HALVES):
+            part = held(f"v_codes2_{h}", [P, HALF], U32)
+            nc.vector.tensor_copy(part[:], tab[2][:].bitcast(U32).indirect(entries(h * HALF, HALF)))
+            v_codes[2, h] = part[:]
+        quantize_wa(2, nc.scalar.copy)
         wo_codes = place("wo_codes", [P, N], I32)
         nc.sync.dma_start(wo_codes[:], wo_words[0].rearrange("p c i -> p (c i)").bitcast(I32))
 
@@ -246,7 +244,6 @@ def tile_list_gated_neighbor_messages_kernel(
         take_banks("content", 0)
         for a in range(PASSES):
             gate_pass(0, a)
-        for a in range(PASSES):
             content_pass(0, a)
         apply_sigmoid(0)
         gained = place("gained", [P, PACK, HALF], F32)
@@ -280,7 +277,6 @@ def tile_list_gated_neighbor_messages_kernel(
         picked[3, 1] = last[:]
         scale_state(0)
         apply_tanh(1)
-        scale_state(1)
 
         out_rows = out.rearrange("(c p) j -> p c j", p=P)
 
@@ -344,6 +340,7 @@ def tile_list_gated_neighbor_messages_kernel(
 
         GROUP = HALF // 2
         gated = {g0: gate_content(g0, GROUP) for g0 in (0, GROUP)}
+        scale_state(1)
         gather_last_state(0, GROUP)
         j0 = 0
         for width in PIECES:

@@ -29,23 +29,27 @@ PIECES = (256, 256, 256, 128, 128)
 KIB = 1024
 LAP = 64
 ROWS = (
-    (("v_codes1", 4 * KIB), ("wb_sc_raw", 1536), ("tab2", 8 * KIB)),
+    (("v_codes1", 4 * KIB), ("wb_sc_raw", 1536)),
     (("v_sc", KIB), ("tab0", 8 * KIB), ("wa_raw2", 8 * KIB), ("gate", 16 * KIB)),
     (("g_tab0", 8 * KIB), ("tab1", 8 * KIB), ("g_tab1", 8 * KIB)),
     (("g_tab2", 8 * KIB), ("wa_raw0", 8 * KIB)),
     (("g_tab3", 8 * KIB), ("wa_raw1", 8 * KIB)),
-    (("tab_sc", 2 * KIB), ("wb_sc", 1536)),
+    (("tab2", 8 * KIB), ("tab_sc", 2 * KIB), ("wb_sc", 1536)),
     (("state0", 8 * KIB), ("wb_codes", 3 * KIB)),
     (("picked2_0", 2 * KIB), ("content1", 8 * KIB)),
     (("gained", 8 * KIB), ("state1", 8 * KIB)),
-    (("gated0", 4 * KIB),),
-    (("gated256", 4 * KIB),),
+    (("gated0", 8 * KIB),),
+    (("h_grouped0", 2 * KIB), ("gated512", 4 * KIB)),
+    (("v_codes2_0", 2 * KIB), ("grouped2", 4 * KIB), ("v_codes2_1", 2 * KIB)),
 )
 INSIDE = {
+    "staged0": ("wa_raw0", KIB),
+    "staged256": ("wa_raw1", KIB),
+    "staged512": ("tab1", KIB),
+    "staged768": ("tab0", KIB),
+    "staged896": ("tab0", 4 * KIB),
     "wo_codes": ("wa_raw2", 2 * KIB),
-    "wa_codes2": ("tab2", KIB),
-    "gated512": ("gated0", 0),
-    "gated768": ("gated256", 0),
+    "gated768": ("gated0", 0),
 }
 
 
@@ -57,7 +61,6 @@ def tile_list_gated_neighbor_messages_kernel(
         lists = ctx.enter_context(tc.tile_pool(name="lists", bufs=1))
         keep = ctx.enter_context(tc.tile_pool(name="keep", bufs=1))
         ring2 = ctx.enter_context(tc.tile_pool(name="ring2", bufs=2))
-        ring3 = ctx.enter_context(tc.tile_pool(name="ring3", bufs=3))
         psum = ctx.enter_context(tc.psum_pool(name="psum", bufs=8))
         placed = ctx.enter_context(tc.tile_pool(name="placed", bufs=1))
         offsets = lists.tile([P, S // LIST_ROWS], U16, name="offsets")
@@ -159,38 +162,38 @@ def tile_list_gated_neighbor_messages_kernel(
             nc.sync.dma_start(
                 v_sc_low[0:SHIFT_ROWS, a - 1, :], v_sc[4 * a : 4 * a + SHIFT_ROWS, :].bitcast(I32)
             )
+        load_tab(2)
         wb_sc = place("wb_sc", [P, PASSES * H], U8)
         nc.vector.tensor_copy(
             wb_sc[:].rearrange("p (t c i) -> p c t i", t=PACK, i=16),
             wb_sc_raw[:].bitcast(U8).rearrange("p a (c i t) -> p (a c) t i", t=PACK, i=16),
         )
-        load_tab(2)
         gather_words(1, place("v_codes1", [P, S], U32))
         load_g(0)
         load_g(1)
 
         wa_codes = [held("wa_codes0", [P, H], U32), held("wa_codes1", [P, H], U32),
-                    place("wa_codes2", [P, H], U32)]
+                    held("wa_codes2", [P, H], U32)]
         wa_sc = [held(f"wa_sc{a}", [P, H], U8) for a in range(PASSES)]
 
-        def quantize_wa(a, copy):
-            grouped = held(f"grouped{a}", [P, H * PACK], BF16)
-            for t0 in range(0, PACK, 2):
+        def quantize_wa(a, copies):
+            grouped = (held, held, place)[a](f"grouped{a}", [P, H * PACK], BF16)
+            for t0, copy in zip((0, 2), copies):
                 copy(
                     grouped[:].rearrange("p (t m j) -> p m j t", t=PACK, j=PACK)[:, :, :, t0 : t0 + 2],
                     wa_raw[a][:].rearrange("p j (m t) -> p m j t", t=PACK)[:, :, :, t0 : t0 + 2],
                 )
             nc.vector.quantize_mx(out=wa_codes[a][:].bitcast(FP8X4), scales=wa_sc[a][:], in_=grouped[:])
 
-        quantize_wa(0, nc.scalar.copy)
+        quantize_wa(0, (nc.scalar.copy, nc.scalar.copy))
         load_g(2)
-        quantize_wa(1, nc.scalar.copy)
+        quantize_wa(1, (nc.scalar.copy, nc.scalar.copy))
         load_g(3)
+        quantize_wa(2, (nc.scalar.copy, nc.vector.tensor_copy))
         for h in range(HALVES):
-            part = held(f"v_codes2_{h}", [P, HALF], U32)
+            part = place(f"v_codes2_{h}", [P, HALF], U32)
             nc.vector.tensor_copy(part[:], tab[2][:].bitcast(U32).indirect(entries(h * HALF, HALF)))
             v_codes[2, h] = part[:]
-        quantize_wa(2, nc.scalar.copy)
         wo_codes = place("wo_codes", [P, N], I32)
         nc.sync.dma_start(wo_codes[:], wo_words[0].rearrange("p c i -> p (c i)").bitcast(I32))
 
@@ -281,18 +284,14 @@ def tile_list_gated_neighbor_messages_kernel(
         out_rows = out.rearrange("(c p) j -> p c j", p=P)
 
         def gate_content(j0, width):
-            h, c0 = divmod(j0, HALF)
-            cols = slice(c0, c0 + width)
+            cols = slice(j0 - HALF, j0 - HALF + width)
             gated = place(f"gated{j0}", [P, PACK, width], F32)
             for t in range(PACK):
-                if h == 0:
-                    nc.gpsimd.tensor_tensor(gated[:, t, :], content[h][:, t, cols], gained[:, t, cols], ALU.mult)
-                else:
-                    nc.vector.scalar_tensor_tensor(
-                        gated[:, t, :], content[h][:, t, cols], gain4[:, t : t + 1],
-                        gate[:, PACK * h + t, cols], ALU.mult, ALU.mult,
-                    )
-            return gated
+                nc.vector.scalar_tensor_tensor(
+                    gated[:, t, :], content[1][:, t, cols], gain4[:, t : t + 1],
+                    gate[:, PACK + t, cols], ALU.mult, ALU.mult,
+                )
+            return gated[:]
 
         def gather_last_state(j0, width):
             h, c0 = divmod(j0, HALF)
@@ -303,7 +302,7 @@ def tile_list_gated_neighbor_messages_kernel(
 
         def sum_h(gated, g0, j0, width):
             h, c0 = divmod(j0, HALF)
-            h_grouped = ring2.tile([P, width * PACK], BF16, name="h_grouped", align_bytes=64)
+            h_grouped = (held if j0 else place)(f"h_grouped{j0}", [P, width * PACK], BF16)
             nc.vector.tensor_tensor(
                 h_grouped[:].rearrange("p (c i t) -> p c t i", i=2, t=PACK),
                 gated[:, :, j0 - g0 : j0 - g0 + width].rearrange("p t (c i) -> p c t i", i=2),
@@ -316,7 +315,7 @@ def tile_list_gated_neighbor_messages_kernel(
             h_codes = ring2.tile([P, width], U32, name="h_codes", align_bytes=64)
             h_sc = ring2.tile([P, width], U8, name="h_sc", align_bytes=64)
             nc.vector.quantize_mx(out=h_codes[:].bitcast(FP8X4), scales=h_sc[:], in_=h_grouped[:])
-            staged = ring3.tile([P, CHUNKS, width], F32, name="staged")
+            staged = place(f"staged{j0}", [P, CHUNKS, width], F32)
             per_bank = min(HALF // width, CHUNKS // 2)
             for c0 in range(0, CHUNKS, per_bank):
                 chunks = slice(c0, c0 + per_bank)
@@ -332,14 +331,19 @@ def tile_list_gated_neighbor_messages_kernel(
                         start=True,
                         stop=True,
                     )
-                if j0 + width == S and c0 > 0:
+                if j0 >= S - HALF // 2 and (c0 > 0 or j0 + width < S):
                     nc.vector.tensor_copy(staged[:, chunks, :], bank[:])
                 else:
                     nc.scalar.copy(staged[:, chunks, :], bank[:])
                 nc.sync.dma_start(out_rows[:, chunks, j0 : j0 + width], staged[:, chunks, :])
 
         GROUP = HALF // 2
-        gated = {g0: gate_content(g0, GROUP) for g0 in (0, GROUP)}
+        first = place("gated0", [P, PACK, HALF], F32)
+        for t0 in range(0, PACK, 2):
+            nc.gpsimd.tensor_tensor(
+                first[:, t0 : t0 + 2, :], content[0][:, t0 : t0 + 2, :], gained[:, t0 : t0 + 2, :], ALU.mult
+            )
+        gated = {g0: first[:, :, g0 : g0 + GROUP] for g0 in (0, GROUP)}
         scale_state(1)
         gather_last_state(0, GROUP)
         j0 = 0

@@ -25,31 +25,30 @@ CHUNKS = N // P
 QUADS = 4
 LIST_ROWS = 16
 SHIFT_ROWS = 112
-PIECES = (256, 256, 256, 128, 128)
+PIECE = 128
 KIB = 1024
 LAP = 64
 ROWS = (
-    (("v_codes1", 4 * KIB), ("wb_sc_raw", 1536)),
-    (("v_sc", KIB), ("tab0", 8 * KIB), ("wa_raw2", 8 * KIB), ("gate", 16 * KIB)),
-    (("g_tab0", 8 * KIB), ("tab1", 8 * KIB), ("g_tab1", 8 * KIB)),
-    (("g_tab2", 8 * KIB), ("wa_raw0", 8 * KIB)),
-    (("g_tab3", 8 * KIB), ("wa_raw1", 8 * KIB)),
-    (("tab2", 8 * KIB), ("tab_sc", 2 * KIB), ("wb_sc", 1536)),
-    (("state0", 8 * KIB), ("wb_codes", 3 * KIB)),
-    (("picked2_0", 2 * KIB), ("content1", 8 * KIB)),
-    (("gained", 8 * KIB), ("state1", 8 * KIB)),
-    (("gated0", 8 * KIB),),
-    (("h_grouped0", 2 * KIB), ("gated512", 4 * KIB)),
-    (("v_codes2_0", 2 * KIB), ("grouped2", 4 * KIB), ("v_codes2_1", 2 * KIB)),
+    (("tab0", 8 * KIB),),
+    (("v_codes0", 4 * KIB), ("tab_sc", 2 * KIB), ("wa_raw1", 8 * KIB), ("g_tab2", 8 * KIB)),
+    (("wa_raw0", 8 * KIB),),
+    (("gate0", 8 * KIB),),
+    (("wa_raw2", 8 * KIB), ("tab1", 8 * KIB)),
+    (("g_tab0", 8 * KIB), ("tab2", 8 * KIB)),
+    (("g_tab1", 8 * KIB), ("grouped0", 4 * KIB)),
+    (("g_tab3", 8 * KIB), ("grouped1", 4 * KIB)),
+    (("gained_late", 4 * KIB), ("grouped2", 4 * KIB), ("wo_codes", 3 * KIB)),
+    (("state0", 4 * KIB), ("v_codes2_1", 2 * KIB), ("state512", 8 * KIB)),
+    (("wb_sc_raw", 1536),),
+    (("gated768", 4 * KIB), ("state256", 4 * KIB), ("content0", 8 * KIB)),
 )
 INSIDE = {
-    "staged0": ("wa_raw0", KIB),
-    "staged256": ("wa_raw1", KIB),
-    "staged512": ("tab1", KIB),
-    "staged768": ("tab0", KIB),
-    "staged896": ("tab0", 4 * KIB),
-    "wo_codes": ("wa_raw2", 2 * KIB),
-    "gated768": ("gated0", 0),
+    "gain4": ("tab1", 512),
+    "wo_sc": ("grouped2", KIB),
+    "staged0": ("tab0", KIB),
+    "staged256": ("tab1", KIB),
+    "staged512": ("tab2", KIB),
+    "staged768": ("wa_raw1", KIB),
 }
 
 
@@ -81,9 +80,7 @@ def tile_list_gated_neighbor_messages_kernel(
             return placed.tile(shape, dtype, name=name, align_bytes=64, offset=at[name])
 
         tab_sc = place("tab_sc", [P, T // 4], I32)
-        wo_sc = held("wo_sc", [P, N // 4], I32)
         v_sc_low = held("v_sc_low", [P, PASSES - 1, S // 4], I32)
-        gain4 = held("gain4", [P, PACK], F32)
         warm_in = held("warm_in", [P, 8], F32)
         warm_out = held("warm_out", [P, 8], F32)
 
@@ -91,7 +88,6 @@ def tile_list_gated_neighbor_messages_kernel(
         nc.gpsimd.memset(tab_sc[:], 0)
         nc.vector.memset(wb_sc_raw[:], 0)
         nc.vector.memset(warm_in[:], 0.0)
-        nc.vector.memset(wo_sc[:], 0)
         nc.vector.memset(v_sc_low[:], 0)
 
         tab, wa_raw, g_tab = {}, {}, {}
@@ -117,29 +113,24 @@ def tile_list_gated_neighbor_messages_kernel(
             )
 
         nc.sync.dma_start(offsets[:], offs)
-        wb_raw = held("wb_raw", [P, PASSES, H // 2], I32)
-        nc.sync.dma_start(wb_raw[:], wb_words.rearrange("a p c -> p a c").bitcast(I32))
         load_tab(0)
         for q in range(QUADS):
             load_tab_scales(q, (nc.sync, nc.scalar)[q // 2])
         load_tab(1)
+        wb_raw = held("wb_raw", [P, PASSES, H // 2], I32)
+        nc.sync.dma_start(wb_raw[:], wb_words.rearrange("a p c -> p a c").bitcast(I32))
         for q in range(QUADS):
             nc.sync.dma_start(
                 wb_sc_raw[32 * q : 32 * q + 4, :, :],
                 wb_scales[:, 4 * q : 4 * q + 4, :].rearrange("a r c -> r a c").bitcast(I32),
             )
+        load_tab(2)
         load_wa(0)
-        load_wa(1)
-        nc.gpsimd.dma_start(gain4[:], gain.rearrange("(p t) -> p t", t=PACK))
-        for q in range(QUADS):
-            nc.gpsimd.dma_start(
-                wo_sc[32 * q : 32 * q + 4, :], wo_scales[0, 4 * q : 4 * q + 4, :].bitcast(I32)
-            )
 
         nc.scalar.activation(warm_out[:], warm_in[:], ACT.Sigmoid)
 
-        wb_codes = place("wb_codes", [P, PASSES * H // 2], I32)
-        nc.vector.tensor_copy(
+        wb_codes = held("wb_codes", [P, PASSES * H // 2], I32)
+        nc.scalar.copy(
             wb_codes[:].bitcast(U16).rearrange("p (t c i) -> p c t i", t=PACK, i=8),
             wb_raw[:].bitcast(U16).rearrange("p a (c i t) -> p (a c) t i", t=PACK, i=8),
         )
@@ -154,73 +145,91 @@ def tile_list_gated_neighbor_messages_kernel(
         def entries(j0, width):
             return offsets[:, j0 // LIST_ROWS : (j0 + width) // LIST_ROWS]
 
-        gather_words(0, held("v_codes0", [P, S], U32))
-        load_wa(2)
-        v_sc = place("v_sc", [P, S], U8)
+        wb_sc = [held(f"wb_sc{a}", [P, H], U8) for a in range(PASSES)]
+        for a in range(PASSES):
+            nc.gpsimd.tensor_copy(
+                wb_sc[a][:].rearrange("p (t m) -> p t m", t=PACK),
+                wb_sc_raw[:, a, :].bitcast(U8).rearrange("p (m t) -> p t m", t=PACK),
+            )
+        v_sc = held("v_sc", [P, S], U8)
         nc.vector.tensor_copy(v_sc[:], tab_sc[:].bitcast(U8).indirect(offsets[:]))
         for a in range(1, PASSES):
             nc.sync.dma_start(
                 v_sc_low[0:SHIFT_ROWS, a - 1, :], v_sc[4 * a : 4 * a + SHIFT_ROWS, :].bitcast(I32)
             )
-        load_tab(2)
-        wb_sc = place("wb_sc", [P, PASSES * H], U8)
-        nc.vector.tensor_copy(
-            wb_sc[:].rearrange("p (t c i) -> p c t i", t=PACK, i=16),
-            wb_sc_raw[:].bitcast(U8).rearrange("p a (c i t) -> p (a c) t i", t=PACK, i=16),
-        )
-        gather_words(1, place("v_codes1", [P, S], U32))
-        load_g(0)
-        load_g(1)
-
-        wa_codes = [held("wa_codes0", [P, H], U32), held("wa_codes1", [P, H], U32),
-                    held("wa_codes2", [P, H], U32)]
-        wa_sc = [held(f"wa_sc{a}", [P, H], U8) for a in range(PASSES)]
-
-        def quantize_wa(a, copies):
-            grouped = (held, held, place)[a](f"grouped{a}", [P, H * PACK], BF16)
-            for t0, copy in zip((0, 2), copies):
-                copy(
-                    grouped[:].rearrange("p (t m j) -> p m j t", t=PACK, j=PACK)[:, :, :, t0 : t0 + 2],
-                    wa_raw[a][:].rearrange("p j (m t) -> p m j t", t=PACK)[:, :, :, t0 : t0 + 2],
-                )
-            nc.vector.quantize_mx(out=wa_codes[a][:].bitcast(FP8X4), scales=wa_sc[a][:], in_=grouped[:])
-
-        quantize_wa(0, (nc.scalar.copy, nc.scalar.copy))
-        load_g(2)
-        quantize_wa(1, (nc.scalar.copy, nc.scalar.copy))
-        load_g(3)
-        quantize_wa(2, (nc.scalar.copy, nc.vector.tensor_copy))
+        load_wa(1)
+        gather_words(0, place("v_codes0", [P, S], U32))
+        gather_words(1, held("v_codes1", [P, S], U32))
+        load_wa(2)
+        gain4 = place("gain4", [P, PACK], F32)
+        nc.sync.dma_start(gain4[:], gain.rearrange("(p t) -> p t", t=PACK))
         for h in range(HALVES):
-            part = place(f"v_codes2_{h}", [P, HALF], U32)
+            part = (held, place)[h](f"v_codes2_{h}", [P, HALF], U32)
             nc.vector.tensor_copy(part[:], tab[2][:].bitcast(U32).indirect(entries(h * HALF, HALF)))
             v_codes[2, h] = part[:]
+        load_g(0)
+
+        wa_codes = [held(f"wa_codes{a}", [P, H], U32) for a in range(PASSES)]
+        wa_sc = [held(f"wa_sc{a}", [P, H], U8) for a in range(PASSES)]
+
+        def round_pair(copy):
+            def run(grouped, raw, t0):
+                copy(
+                    grouped[:].rearrange("p (t m j) -> p m j t", t=PACK, j=PACK)[:, :, :, t0 : t0 + 2],
+                    raw[:].rearrange("p j (m t) -> p m j t", t=PACK)[:, :, :, t0 : t0 + 2],
+                )
+
+            return run
+
+        def round_pair_gpsimd(grouped, raw, t0):
+            nc.gpsimd.tensor_copy(
+                grouped[:].rearrange("p (t m j) -> p t m j", t=PACK, j=PACK)[:, t0 : t0 + 2, :, :],
+                raw[:].rearrange("p j (m t) -> p t m j", t=PACK)[:, t0 : t0 + 2, :, :],
+            )
+
+        on_scalar, on_vector = round_pair(nc.scalar.copy), round_pair(nc.vector.tensor_copy)
+
+        def quantize_wa(a, rounders):
+            grouped = place(f"grouped{a}", [P, H * PACK], BF16)
+            for t0, rounder in zip((0, 2), rounders):
+                rounder(grouped, wa_raw[a], t0)
+            nc.vector.quantize_mx(out=wa_codes[a][:].bitcast(FP8X4), scales=wa_sc[a][:], in_=grouped[:])
+
+        quantize_wa(0, (on_scalar, round_pair_gpsimd))
+        load_g(1)
+        quantize_wa(1, (on_vector, on_vector))
+        load_g(2)
+        load_g(3)
+        quantize_wa(2, (on_vector, on_vector))
         wo_codes = place("wo_codes", [P, N], I32)
         nc.sync.dma_start(wo_codes[:], wo_words[0].rearrange("p c i -> p (c i)").bitcast(I32))
+        wo_sc = place("wo_sc", [P, N // 4], I32)
+        nc.gpsimd.memset(wo_sc[:], 0)
+        for q in range(QUADS):
+            nc.sync.dma_start(
+                wo_sc[32 * q : 32 * q + 4, :], wo_scales[0, 4 * q : 4 * q + 4, :].bitcast(I32)
+            )
 
-        gate = place("gate", [P, HALVES * PACK, HALF], F32)
-        gain_wide = held("gain_wide", [P, HALF // 2], F32)
-        nc.scalar.copy(gain_wide[:], gain4[:, PACK - 1 :].to_broadcast([P, HALF // 2]))
+        banks, gate, content = {}, {}, {}
 
-        banks, content, state, picked = {}, {}, {}, {}
-
-        def gate_pass(h, a):
+        def gate_pass(h, a, planes):
             cols = slice(h * HALF, (h + 1) * HALF)
             low = v_sc[:, cols] if a == 0 else v_sc_low[:, a - 1, :].bitcast(U8)[:, cols]
-            for t in range(PACK):
+            for t in planes:
                 m0 = P * (PASSES * t + a)
                 nc.tensor.matmul_mx(
                     out=banks["gate", h][t][:],
                     lhsT=wb_codes[:].bitcast(U8)[:, 2 * m0 : 2 * (m0 + P)].bitcast(FP4X4),
-                    lhsT_scale=wb_sc[:, m0 : m0 + P],
+                    lhsT_scale=wb_sc[a][:, P * t : P * (t + 1)],
                     rhs=v_codes[a, h].bitcast(FP8X4),
                     rhs_scale=low,
                     start=(a == 0),
                     stop=(a == PASSES - 1),
                 )
 
-        def content_pass(h, a):
+        def content_pass(h, a, planes):
             cols = slice(h * HALF, (h + 1) * HALF)
-            for t in range(PACK):
+            for t in planes:
                 nc.tensor.matmul_mx(
                     out=banks["content", h][t][:],
                     lhsT=wa_codes[a][:, P * t : P * (t + 1)].bitcast(FP8X4),
@@ -234,92 +243,98 @@ def tile_list_gated_neighbor_messages_kernel(
         def take_banks(kind, h):
             banks[kind, h] = [psum.tile([P, HALF], F32, name="bank") for t in range(PACK)]
 
-        def apply_sigmoid(h):
+        def activate(kind, h, func, into):
+            into[h] = (place if (kind, h) == ("gate", 0) else held)(f"{kind}{h}", [P, PACK, HALF], F32)
             for t in range(PACK):
-                nc.scalar.activation(gate[:, PACK * h + t, :], banks["gate", h][t][:], ACT.Sigmoid)
+                nc.scalar.activation(into[h][:, t, :], banks[kind, h][t][:], func)
 
-        def apply_tanh(h):
-            content[h] = (held, place)[h](f"content{h}", [P, PACK, HALF], F32)
+        for h in range(HALVES):
+            take_banks("gate", h)
+        for h in range(HALVES):
+            gate_pass(h, 0, range(PACK))
             for t in range(PACK):
-                nc.scalar.activation(content[h][:, t, :], banks["content", h][t][:], ACT.Tanh)
-
-        take_banks("gate", 0)
+                for a in range(1, PASSES):
+                    gate_pass(h, a, (t,))
+        for h in range(HALVES):
+            activate("gate", h, ACT.Sigmoid, gate)
+        GROUP = HALF // 2
+        gained = held("gained", [P, PACK, HALF], F32)
+        gained_third = place("gained_late", [P, PACK, GROUP], F32)
+        for t in range(PACK):
+            nc.gpsimd.tensor_scalar(
+                gained_third[:, t, :], gate[1][:, t, :GROUP], gain4[:, t : t + 1], 0.0, ALU.mult, ALU.add
+            )
         take_banks("content", 0)
         for a in range(PASSES):
-            gate_pass(0, a)
-            content_pass(0, a)
-        apply_sigmoid(0)
-        gained = place("gained", [P, PACK, HALF], F32)
+            content_pass(0, a, range(PACK))
+        content[0] = place("content0", [P, PACK, HALF], F32)
+
+        def gain_gate(t):
+            nc.scalar.activation(gained[:, t, :], gate[0][:, t, :], ACT.Copy, scale=gain4[:, t : t + 1])
+
+        for t in range(PACK - 1):
+            gain_gate(t)
         for t in range(PACK):
-            nc.gpsimd.tensor_scalar(gained[:, t, :], gate[:, t, :], gain4[:, t : t + 1], 0.0, ALU.mult, ALU.add)
-        apply_tanh(0)
-        take_banks("gate", 1)
-        for a in range(PASSES):
-            gate_pass(1, a)
-        apply_sigmoid(1)
+            if t == 2:
+                gain_gate(PACK - 1)
+            nc.scalar.activation(content[0][:, t, :], banks["content", 0][t][:], ACT.Tanh)
         take_banks("content", 1)
-        for a in range(PASSES):
-            content_pass(1, a)
+        for t in range(PACK):
+            for a in range(PASSES):
+                content_pass(1, a, (t,))
+        activate("content", 1, ACT.Tanh, content)
+        first = held("gated0", [P, PACK, HALF], F32)
+        for t0 in (0, 2):
+            nc.gpsimd.tensor_tensor(
+                first[:, t0 : t0 + 2, :], content[0][:, t0 : t0 + 2, :], gained[:, t0 : t0 + 2, :], ALU.mult
+            )
+        third = held("gated512", [P, PACK, GROUP], F32)
+        nc.gpsimd.tensor_tensor(third[:], content[1][:, :, :GROUP], gained_third[:], ALU.mult)
 
-        def scale_state(h):
-            state[h] = place(f"state{h}", [P, PACK, HALF], F32)
-            for t in range(PACK - 1 + h):
-                nc.scalar.activation(state[h][:, t, :], picked[t, h], ACT.Copy, scale=gain4[:, t : t + 1])
-
-        for t in range(PACK - 2):
+        picked, state = {}, {}
+        for t in range(PACK - 1):
             whole = held(f"picked{t}", [P, S], F32)
             nc.vector.tensor_copy(whole[:], g_tab[t][:].indirect(offsets[:]))
             for h in range(HALVES):
                 picked[t, h] = whole[:, h * HALF : (h + 1) * HALF]
         for h in range(HALVES):
-            part = (place, held)[h](f"picked2_{h}", [P, HALF], F32)
-            nc.vector.tensor_copy(part[:], g_tab[2][:].indirect(entries(h * HALF, HALF)))
-            picked[2, h] = part[:]
-        last = held("picked3_1", [P, HALF], F32)
-        nc.vector.tensor_copy(last[:], g_tab[3][:].indirect(entries(HALF, HALF)))
-        picked[3, 1] = last[:]
-        scale_state(0)
-        apply_tanh(1)
+            part = held(f"picked3_{h}", [P, HALF], F32)
+            nc.vector.tensor_copy(part[:], g_tab[3][:].indirect(entries(h * HALF, HALF)))
+            picked[3, h] = part[:]
+        scaled = {}
+
+        def scale_state(g0, width, planes):
+            h, c0 = divmod(g0, HALF)
+            if g0 not in scaled:
+                scaled[g0] = place(f"state{g0}", [P, PACK, width], F32)
+                for c in range(0, width, GROUP):
+                    state[g0 + c] = scaled[g0][:, :, c : c + GROUP]
+            for t in planes:
+                nc.scalar.activation(
+                    scaled[g0][:, t, :], picked[t, h][:, c0 : c0 + width], ACT.Copy, scale=gain4[:, t : t + 1]
+                )
+
+        scale_state(0, GROUP, range(PACK - 1))
+        scale_state(HALF, HALF, range(PACK - 1))
+        scale_state(0, GROUP, (PACK - 1,))
+        scale_state(GROUP, GROUP, range(PACK))
+        scale_state(HALF, HALF, (PACK - 1,))
 
         out_rows = out.rearrange("(c p) j -> p c j", p=P)
+        staged = {}
 
-        def gate_content(j0, width):
-            cols = slice(j0 - HALF, j0 - HALF + width)
-            gated = place(f"gated{j0}", [P, PACK, width], F32)
-            for t in range(PACK):
-                nc.vector.scalar_tensor_tensor(
-                    gated[:, t, :], content[1][:, t, cols], gain4[:, t : t + 1],
-                    gate[:, PACK + t, cols], ALU.mult, ALU.mult,
-                )
-            return gated[:]
-
-        def gather_last_state(j0, width):
-            h, c0 = divmod(j0, HALF)
-            nc.vector.tensor_tensor(
-                state[h][:, PACK - 1, c0 : c0 + width], g_tab[PACK - 1][:].indirect(entries(j0, width)),
-                gain_wide[:, :width], ALU.mult,
-            )
-
-        def sum_h(gated, g0, j0, width):
-            h, c0 = divmod(j0, HALF)
-            h_grouped = (held if j0 else place)(f"h_grouped{j0}", [P, width * PACK], BF16)
-            nc.vector.tensor_tensor(
-                h_grouped[:].rearrange("p (c i t) -> p c t i", i=2, t=PACK),
-                gated[:, :, j0 - g0 : j0 - g0 + width].rearrange("p t (c i) -> p c t i", i=2),
-                state[h][:, :, c0 : c0 + width].rearrange("p t (c i) -> p c t i", i=2),
-                ALU.add,
-            )
-            return h_grouped
-
-        def project(h_grouped, j0, width):
-            h_codes = ring2.tile([P, width], U32, name="h_codes", align_bytes=64)
-            h_sc = ring2.tile([P, width], U8, name="h_sc", align_bytes=64)
+        def project(h_grouped, j0):
+            g0 = j0 - j0 % GROUP
+            h_codes = ring2.tile([P, PIECE], U32, name="h_codes", align_bytes=64)
+            h_sc = ring2.tile([P, PIECE], U8, name="h_sc", align_bytes=64)
             nc.vector.quantize_mx(out=h_codes[:].bitcast(FP8X4), scales=h_sc[:], in_=h_grouped[:])
-            staged = place(f"staged{j0}", [P, CHUNKS, width], F32)
-            per_bank = min(HALF // width, CHUNKS // 2)
+            if j0 == g0:
+                staged[g0] = place(f"staged{g0}", [P, CHUNKS, GROUP], F32)
+            cols = slice(j0 - g0, j0 - g0 + PIECE)
+            per_bank = CHUNKS // 2
             for c0 in range(0, CHUNKS, per_bank):
                 chunks = slice(c0, c0 + per_bank)
-                bank = psum.tile([P, per_bank, width], F32, name="bank")
+                bank = psum.tile([P, per_bank, PIECE], F32, name="bank")
                 for u in range(per_bank):
                     n_cols = slice(P * (c0 + u), P * (c0 + u + 1))
                     nc.tensor.matmul_mx(
@@ -331,28 +346,32 @@ def tile_list_gated_neighbor_messages_kernel(
                         start=True,
                         stop=True,
                     )
-                if j0 >= S - HALF // 2 and (c0 > 0 or j0 + width < S):
-                    nc.vector.tensor_copy(staged[:, chunks, :], bank[:])
+                if g0 == S - GROUP and c0 > 0:
+                    nc.vector.tensor_copy(staged[g0][:, chunks, cols], bank[:])
                 else:
-                    nc.scalar.copy(staged[:, chunks, :], bank[:])
-                nc.sync.dma_start(out_rows[:, chunks, j0 : j0 + width], staged[:, chunks, :])
+                    nc.scalar.copy(staged[g0][:, chunks, cols], bank[:])
+                if g0 == S - GROUP:
+                    nc.sync.dma_start(out_rows[:, chunks, j0 : j0 + PIECE], staged[g0][:, chunks, cols])
+                elif j0 > g0:
+                    nc.sync.dma_start(out_rows[:, chunks, g0 : g0 + GROUP], staged[g0][:, chunks, :])
 
-        GROUP = HALF // 2
-        first = place("gated0", [P, PACK, HALF], F32)
-        for t0 in range(0, PACK, 2):
-            nc.gpsimd.tensor_tensor(
-                first[:, t0 : t0 + 2, :], content[0][:, t0 : t0 + 2, :], gained[:, t0 : t0 + 2, :], ALU.mult
-            )
-        gated = {g0: first[:, :, g0 : g0 + GROUP] for g0 in (0, GROUP)}
-        scale_state(1)
-        gather_last_state(0, GROUP)
-        j0 = 0
-        for width in PIECES:
+        gated = {0: first[:, :, :GROUP], GROUP: first[:, :, GROUP:], HALF: third[:]}
+        for j0 in range(0, S, PIECE):
             g0 = j0 - j0 % GROUP
-            h_grouped = sum_h(gated[g0], g0, j0, width)
-            if j0 == g0 and g0 + GROUP < HALF:
-                gather_last_state(g0 + GROUP, GROUP)
-            project(h_grouped, j0, width)
-            if j0 + width == g0 + GROUP and g0 + 2 * GROUP < S:
-                gated[g0 + 2 * GROUP] = gate_content(g0 + 2 * GROUP, GROUP)
-            j0 += width
+            cols = slice(j0 - g0, j0 - g0 + PIECE)
+            if j0 == S - GROUP:
+                last = place(f"gated{j0}", [P, PACK, GROUP], F32)
+                for t in range(PACK):
+                    nc.vector.scalar_tensor_tensor(
+                        last[:, t, :], content[1][:, t, GROUP:], gain4[:, t : t + 1],
+                        gate[1][:, t, GROUP:], ALU.mult, ALU.mult,
+                    )
+                gated[j0] = last[:]
+            h_grouped = held(f"h_grouped{j0}", [P, PIECE * PACK], BF16)
+            nc.vector.tensor_tensor(
+                h_grouped[:].rearrange("p (c i t) -> p c t i", i=2, t=PACK),
+                gated[g0][:, :, cols].rearrange("p t (c i) -> p c t i", i=2),
+                state[g0][:, :, cols].rearrange("p t (c i) -> p c t i", i=2),
+                ALU.add,
+            )
+            project(h_grouped, j0)

@@ -30,7 +30,7 @@ KIB = 1024
 LAP = 64
 ROWS = (
     (("tab0", 8 * KIB),),
-    (("v_codes0", 4 * KIB), ("tab_sc", 2 * KIB), ("wa_raw1", 8 * KIB), ("g_tab2", 8 * KIB)),
+    (("v_codes0_1", 2 * KIB), ("tab_sc", 2 * KIB), ("wa_raw1", 8 * KIB), ("g_tab2", 8 * KIB)),
     (("wa_raw0", 8 * KIB),),
     (("gate0", 8 * KIB),),
     (("wa_raw2", 8 * KIB), ("tab1", 8 * KIB)),
@@ -151,6 +151,11 @@ def tile_list_gated_neighbor_messages_kernel(
                 wb_sc[a][:].rearrange("p (t m) -> p t m", t=PACK),
                 wb_sc_raw[:, a, :].bitcast(U8).rearrange("p (m t) -> p t m", t=PACK),
             )
+        def gather_half(a, h, tile):
+            nc.vector.tensor_copy(tile[:], tab[a][:].bitcast(U32).indirect(entries(h * HALF, HALF)))
+            v_codes[a, h] = tile[:]
+
+        gather_half(0, 0, held("v_codes0_0", [P, HALF], U32))
         v_sc = held("v_sc", [P, S], U8)
         nc.vector.tensor_copy(v_sc[:], tab_sc[:].bitcast(U8).indirect(offsets[:]))
         for a in range(1, PASSES):
@@ -158,15 +163,13 @@ def tile_list_gated_neighbor_messages_kernel(
                 v_sc_low[0:SHIFT_ROWS, a - 1, :], v_sc[4 * a : 4 * a + SHIFT_ROWS, :].bitcast(I32)
             )
         load_wa(1)
-        gather_words(0, place("v_codes0", [P, S], U32))
+        gather_half(0, 1, place("v_codes0_1", [P, HALF], U32))
         gather_words(1, held("v_codes1", [P, S], U32))
         load_wa(2)
         gain4 = place("gain4", [P, PACK], F32)
         nc.sync.dma_start(gain4[:], gain.rearrange("(p t) -> p t", t=PACK))
         for h in range(HALVES):
-            part = (held, place)[h](f"v_codes2_{h}", [P, HALF], U32)
-            nc.vector.tensor_copy(part[:], tab[2][:].bitcast(U32).indirect(entries(h * HALF, HALF)))
-            v_codes[2, h] = part[:]
+            gather_half(2, h, (held, place)[h](f"v_codes2_{h}", [P, HALF], U32))
         load_g(0)
 
         wa_codes = [held(f"wa_codes{a}", [P, H], U32) for a in range(PASSES)]

@@ -43,7 +43,6 @@ ROWS = (
     (("gated768", 4 * KIB), ("state256", 4 * KIB), ("content0", 8 * KIB)),
 )
 INSIDE = {
-    "gain4": ("tab1", 512),
     "wo_sc": ("grouped2", KIB),
     "staged0": ("tab0", KIB),
     "staged256": ("tab1", KIB),
@@ -127,6 +126,9 @@ def tile_list_gated_neighbor_messages_kernel(
         load_tab(2)
         load_wa(0)
 
+        gain4 = held("gain4", [P, PACK], F32)
+        nc.gpsimd.dma_start(gain4[:], gain.rearrange("(p t) -> p t", t=PACK))
+
         nc.scalar.activation(warm_out[:], warm_in[:], ACT.Sigmoid)
 
         wb_codes = held("wb_codes", [P, PASSES * H // 2], I32)
@@ -166,8 +168,6 @@ def tile_list_gated_neighbor_messages_kernel(
         gather_half(0, 1, place("v_codes0_1", [P, HALF], U32))
         gather_words(1, held("v_codes1", [P, S], U32))
         load_wa(2)
-        gain4 = place("gain4", [P, PACK], F32)
-        nc.sync.dma_start(gain4[:], gain.rearrange("(p t) -> p t", t=PACK))
         for h in range(HALVES):
             gather_half(2, h, (held, place)[h](f"v_codes2_{h}", [P, HALF], U32))
         load_g(0)
@@ -196,7 +196,13 @@ def tile_list_gated_neighbor_messages_kernel(
             grouped = place(f"grouped{a}", [P, H * PACK], BF16)
             for t0, rounder in zip((0, 2), rounders):
                 rounder(grouped, wa_raw[a], t0)
-            nc.vector.quantize_mx(out=wa_codes[a][:].bitcast(FP8X4), scales=wa_sc[a][:], in_=grouped[:])
+            parts = 2 if a == PASSES - 1 else 1
+            for c0 in range(0, H, H // parts):
+                cols = slice(c0, c0 + H // parts)
+                nc.vector.quantize_mx(
+                    out=wa_codes[a][:, cols].bitcast(FP8X4), scales=wa_sc[a][:, cols],
+                    in_=grouped[:, PACK * cols.start : PACK * cols.stop],
+                )
 
         quantize_wa(0, (on_scalar, round_pair_gpsimd))
         load_g(1)

@@ -359,7 +359,7 @@ def tile_list_gated_neighbor_messages_kernel(
                     nc.vector.tensor_copy(staged[g0][:, chunks, cols], bank[:])
                 else:
                     nc.scalar.copy(staged[g0][:, chunks, cols], bank[:])
-                if g0 == S - GROUP:
+                if g0 in (0, S - GROUP):
                     nc.sync.dma_start(out_rows[:, chunks, j0 : j0 + PIECE], staged[g0][:, chunks, cols])
                 elif j0 > g0:
                     nc.sync.dma_start(out_rows[:, chunks, g0 : g0 + GROUP], staged[g0][:, chunks, :])

@@ -330,39 +330,50 @@ def tile_list_gated_neighbor_messages_kernel(
         scale_state(HALF, HALF, (PACK - 1,))
 
         out_rows = out.rearrange("(c p) j -> p c j", p=P)
-        staged = {}
+        staged, group_banks = {}, {}
+
+        def multiply(bank, c0, codes, scales):
+            for u in range(bank.shape[1]):
+                n_cols = slice(P * (c0 + u), P * (c0 + u + 1))
+                nc.tensor.matmul_mx(
+                    out=bank[:, u, :],
+                    lhsT=wo_codes[:, n_cols].bitcast(FP8X4),
+                    lhsT_scale=wo_sc[:].bitcast(U8)[:, n_cols],
+                    rhs=codes[:].bitcast(FP8X4),
+                    rhs_scale=scales[:],
+                    start=True,
+                    stop=True,
+                )
+
+        def send(bank, c0, g0, cols, copy):
+            chunks = slice(c0, c0 + bank.shape[1])
+            copy(staged[g0][:, chunks, cols], bank)
+            nc.sync.dma_start(out_rows[:, chunks, g0 + cols.start : g0 + cols.stop], staged[g0][:, chunks, cols])
 
         def project(h_grouped, j0):
             g0 = j0 - j0 % GROUP
+            cols = slice(j0 - g0, j0 - g0 + PIECE)
             h_codes = ring2.tile([P, PIECE], U32, name="h_codes", align_bytes=64)
             h_sc = ring2.tile([P, PIECE], U8, name="h_sc", align_bytes=64)
             nc.vector.quantize_mx(out=h_codes[:].bitcast(FP8X4), scales=h_sc[:], in_=h_grouped[:])
             if j0 == g0:
                 staged[g0] = place(f"staged{g0}", [P, CHUNKS, GROUP], F32)
-            cols = slice(j0 - g0, j0 - g0 + PIECE)
-            per_bank = CHUNKS // 2
-            for c0 in range(0, CHUNKS, per_bank):
-                chunks = slice(c0, c0 + per_bank)
-                bank = psum.tile([P, per_bank, PIECE], F32, name="bank")
-                for u in range(per_bank):
-                    n_cols = slice(P * (c0 + u), P * (c0 + u + 1))
-                    nc.tensor.matmul_mx(
-                        out=bank[:, u, :],
-                        lhsT=wo_codes[:, n_cols].bitcast(FP8X4),
-                        lhsT_scale=wo_sc[:].bitcast(U8)[:, n_cols],
-                        rhs=h_codes[:].bitcast(FP8X4),
-                        rhs_scale=h_sc[:],
-                        start=True,
-                        stop=True,
-                    )
-                if g0 == S - GROUP and c0 > 0:
-                    nc.vector.tensor_copy(staged[g0][:, chunks, cols], bank[:])
-                else:
-                    nc.scalar.copy(staged[g0][:, chunks, cols], bank[:])
-                if g0 in (0, S - GROUP):
-                    nc.sync.dma_start(out_rows[:, chunks, j0 : j0 + PIECE], staged[g0][:, chunks, cols])
-                elif j0 > g0:
-                    nc.sync.dma_start(out_rows[:, chunks, g0 : g0 + GROUP], staged[g0][:, chunks, :])
+            if g0 == 0:
+                for c0 in range(0, CHUNKS, CHUNKS // 2):
+                    bank = psum.tile([P, CHUNKS // 2, PIECE], F32, name="bank")
+                    multiply(bank[:], c0, h_codes, h_sc)
+                    send(bank[:], c0, g0, cols, nc.scalar.copy)
+                return
+            per_bank = HALF // GROUP
+            if j0 == g0:
+                group_banks[g0] = [
+                    psum.tile([P, per_bank, GROUP], F32, name="bank") for c0 in range(0, CHUNKS, per_bank)
+                ]
+            for c0, bank in zip(range(0, CHUNKS, per_bank), group_banks[g0]):
+                multiply(bank[:, :, cols], c0, h_codes, h_sc)
+                if j0 > g0:
+                    on_vector = g0 == S - GROUP and c0 == per_bank
+                    send(bank[:], c0, g0, slice(0, GROUP), nc.vector.tensor_copy if on_vector else nc.scalar.copy)
 
         gated = {0: first[:, :, :GROUP], GROUP: first[:, :, GROUP:], HALF: third[:]}
         for j0 in range(0, S, PIECE):

@@ -40,7 +40,8 @@ ROWS = (
     (("gained_late", 4 * KIB), ("grouped2", 4 * KIB), ("wo_codes", 3 * KIB)),
     (("state0", 4 * KIB), ("v_codes2_1", 2 * KIB), ("state512", 8 * KIB)),
     (("wb_sc_raw", 1536),),
-    (("gated768", 4 * KIB), ("state256", 4 * KIB), ("content0", 8 * KIB)),
+    (("state256", 4 * KIB), ("content0", 8 * KIB)),
+    (("gated768", 2 * KIB), ("h_grouped384", KIB), ("gated896", 2 * KIB)),
 )
 INSIDE = {
     "wo_sc": ("grouped2", KIB),
@@ -111,8 +112,8 @@ def tile_list_gated_neighbor_messages_kernel(
                 tab_sc[32 * q : 32 * q + 4 * PASSES, :], tab_scales[:, 4 * q : 4 * q + 4, :].bitcast(I32)
             )
 
-        nc.sync.dma_start(offsets[:], offs)
         load_tab(0)
+        nc.sync.dma_start(offsets[:], offs)
         for q in range(QUADS):
             load_tab_scales(q, (nc.sync, nc.scalar)[q // 2])
         load_tab(1)
@@ -375,23 +376,30 @@ def tile_list_gated_neighbor_messages_kernel(
                     on_vector = g0 == S - GROUP and c0 == per_bank
                     send(bank[:], c0, g0, slice(0, GROUP), nc.vector.tensor_copy if on_vector else nc.scalar.copy)
 
-        gated = {0: first[:, :, :GROUP], GROUP: first[:, :, GROUP:], HALF: third[:]}
+        def product_on_vector(j0):
+            cols = slice(j0 - HALF, j0 - HALF + PIECE)
+            product = place(f"gated{j0}", [P, PACK, PIECE], F32)
+            for t in range(PACK):
+                nc.vector.scalar_tensor_tensor(
+                    product[:, t, :], content[1][:, t, cols], gain4[:, t : t + 1],
+                    gate[1][:, t, cols], ALU.mult, ALU.mult,
+                )
+            return product[:]
+
+        gated = {j0: first[:, :, j0 : j0 + PIECE] for j0 in range(0, HALF, PIECE)}
+        for c0 in range(0, GROUP, PIECE):
+            gated[HALF + c0] = third[:, :, c0 : c0 + PIECE]
         for j0 in range(0, S, PIECE):
             g0 = j0 - j0 % GROUP
-            cols = slice(j0 - g0, j0 - g0 + PIECE)
             if j0 == S - GROUP:
-                last = place(f"gated{j0}", [P, PACK, GROUP], F32)
-                for t in range(PACK):
-                    nc.vector.scalar_tensor_tensor(
-                        last[:, t, :], content[1][:, t, GROUP:], gain4[:, t : t + 1],
-                        gate[1][:, t, GROUP:], ALU.mult, ALU.mult,
-                    )
-                gated[j0] = last[:]
-            h_grouped = held(f"h_grouped{j0}", [P, PIECE * PACK], BF16)
+                gated[j0] = product_on_vector(j0)
+            h_grouped = (place if j0 == HALF - PIECE else held)(f"h_grouped{j0}", [P, PIECE * PACK], BF16)
             nc.vector.tensor_tensor(
                 h_grouped[:].rearrange("p (c i t) -> p c t i", i=2, t=PACK),
-                gated[g0][:, :, cols].rearrange("p t (c i) -> p c t i", i=2),
-                state[g0][:, :, cols].rearrange("p t (c i) -> p c t i", i=2),
+                gated[j0].rearrange("p t (c i) -> p c t i", i=2),
+                state[g0][:, :, j0 - g0 : j0 - g0 + PIECE].rearrange("p t (c i) -> p c t i", i=2),
                 ALU.add,
             )
+            if j0 == S - GROUP:
+                gated[j0 + PIECE] = product_on_vector(j0 + PIECE)
             project(h_grouped, j0)

@@ -26,6 +26,7 @@ QUADS = 4
 LIST_ROWS = 16
 SHIFT_ROWS = 112
 PIECE = 128
+STORE_ENDS = {256: (2, 4, 6), 512: (2, 6), 768: (4, 6)}
 KIB = 1024
 LAP = 64
 ROWS = (
@@ -346,10 +347,8 @@ def tile_list_gated_neighbor_messages_kernel(
                     stop=True,
                 )
 
-        def send(bank, c0, g0, cols, copy):
-            chunks = slice(c0, c0 + bank.shape[1])
-            copy(staged[g0][:, chunks, cols], bank)
-            nc.sync.dma_start(out_rows[:, chunks, g0 + cols.start : g0 + cols.stop], staged[g0][:, chunks, cols])
+        def store(g0, c0, c1, cols):
+            nc.sync.dma_start(out_rows[:, c0:c1, g0 + cols.start : g0 + cols.stop], staged[g0][:, c0:c1, cols])
 
         def project(h_grouped, j0):
             g0 = j0 - j0 % GROUP
@@ -361,20 +360,30 @@ def tile_list_gated_neighbor_messages_kernel(
                 staged[g0] = place(f"staged{g0}", [P, CHUNKS, GROUP], F32)
             if g0 == 0:
                 for c0 in range(0, CHUNKS, CHUNKS // 2):
+                    c1 = c0 + CHUNKS // 2
                     bank = psum.tile([P, CHUNKS // 2, PIECE], F32, name="bank")
                     multiply(bank[:], c0, h_codes, h_sc)
-                    send(bank[:], c0, g0, cols, nc.scalar.copy)
+                    nc.scalar.copy(staged[g0][:, c0:c1, cols], bank[:])
+                    if j0 == 0:
+                        store(g0, c0, c1, cols)
+                if j0 > 0:
+                    store(g0, 0, CHUNKS, cols)
                 return
             per_bank = HALF // GROUP
             if j0 == g0:
                 group_banks[g0] = [
                     psum.tile([P, per_bank, GROUP], F32, name="bank") for c0 in range(0, CHUNKS, per_bank)
                 ]
+            unsent = 0
             for c0, bank in zip(range(0, CHUNKS, per_bank), group_banks[g0]):
                 multiply(bank[:, :, cols], c0, h_codes, h_sc)
                 if j0 > g0:
+                    c1 = c0 + per_bank
                     on_vector = g0 == S - GROUP and c0 == per_bank
-                    send(bank[:], c0, g0, slice(0, GROUP), nc.vector.tensor_copy if on_vector else nc.scalar.copy)
+                    (nc.vector.tensor_copy if on_vector else nc.scalar.copy)(staged[g0][:, c0:c1, :], bank[:])
+                    if c1 in STORE_ENDS[g0]:
+                        store(g0, unsent, c1, slice(0, GROUP))
+                        unsent = c1
 
         def product_on_vector(j0):
             cols = slice(j0 - HALF, j0 - HALF + PIECE)

@@ -370,12 +370,16 @@ def tile_list_gated_neighbor_messages_kernel(
                     store(g0, 0, CHUNKS, cols)
                 return
             per_bank = HALF // GROUP
+            unsent = per_bank if g0 == S - GROUP else 0
+            if unsent:
+                bank = psum.tile([P, per_bank, PIECE], F32, name="bank")
+                multiply(bank[:], 0, h_codes, h_sc)
+                nc.scalar.copy(staged[g0][:, :per_bank, cols], bank[:])
+                store(g0, 0, per_bank, cols)
+            late = range(unsent, CHUNKS, per_bank)
             if j0 == g0:
-                group_banks[g0] = [
-                    psum.tile([P, per_bank, GROUP], F32, name="bank") for c0 in range(0, CHUNKS, per_bank)
-                ]
-            unsent = 0
-            for c0, bank in zip(range(0, CHUNKS, per_bank), group_banks[g0]):
+                group_banks[g0] = [psum.tile([P, per_bank, GROUP], F32, name="bank") for c0 in late]
+            for c0, bank in zip(late, group_banks[g0]):
                 multiply(bank[:, :, cols], c0, h_codes, h_sc)
                 if j0 > g0:
                     c1 = c0 + per_bank

from contextlib import ExitStack

import concourse.mybir as mybir

K, H, N, T, S = 1536, 512, 768, 2048, 1024
FLOPS = 2 * S * (2 * K * H + H * N)

F32 = mybir.dt.float32
BF16 = mybir.dt.bfloat16
I32 = mybir.dt.int32
U32 = mybir.dt.uint32
U16 = mybir.dt.uint16
U8 = mybir.dt.uint8
FP8X4 = mybir.dt.float8_e4m3fn_x4
FP4X4 = mybir.dt.float4_e2m1fn_x4
ACT = mybir.ActivationFunctionType
ALU = mybir.AluOpType

P = 128
PACK = 4
PASSES = K // (P * PACK)
HALF = 512
HALVES = S // HALF
CHUNKS = N // P
QUADS = 4
LIST_ROWS = 16
SHIFT_ROWS = 112
PIECE = 128
STORE_ENDS = {256: (2, 4, 6), 512: (2, 6), 768: (4, 6)}
KIB = 1024
LAP = 64
ROWS = (
    (("tab0", 8 * KIB),),
    (("v_codes0_1", 2 * KIB), ("tab_sc", 2 * KIB), ("wa_raw1", 8 * KIB), ("g_tab2", 8 * KIB)),
    (("wa_raw0", 8 * KIB),),
    (("gate0", 8 * KIB),),
    (("wa_raw2", 8 * KIB), ("tab1", 8 * KIB)),
    (("g_tab0", 8 * KIB), ("tab2", 8 * KIB)),
    (("g_tab1", 8 * KIB), ("grouped0", 4 * KIB)),
    (("g_tab3", 8 * KIB), ("grouped1", 4 * KIB)),
    (("gained_late", 4 * KIB), ("grouped2", 4 * KIB), ("wo_codes", 3 * KIB)),
    (("state0", 4 * KIB), ("v_codes2_1", 2 * KIB), ("state512", 8 * KIB)),
    (("wb_sc_raw", 1536),),
    (("state256", 4 * KIB), ("content0", 8 * KIB)),
    (("gated768", 2 * KIB), ("h_grouped384", KIB), ("gated896", 2 * KIB)),
)
INSIDE = {
    "wo_sc": ("grouped2", KIB),
    "staged0": ("tab0", KIB),
    "staged256": ("tab1", KIB),
    "staged512": ("tab2", KIB),
    "staged768": ("wa_raw1", KIB),
}


def tile_list_gated_neighbor_messages_kernel(
    tc, tab_words, tab_scales, offs, wa, wb_words, wb_scales, gT, gain, wo_words, wo_scales, out
):
    nc = tc.nc
    with ExitStack() as ctx:
        lists = ctx.enter_context(tc.tile_pool(name="lists", bufs=1))
        keep = ctx.enter_context(tc.tile_pool(name="keep", bufs=1))
        ring2 = ctx.enter_context(tc.tile_pool(name="ring2", bufs=2))
        psum = ctx.enter_context(tc.psum_pool(name="psum", bufs=8))
        placed = ctx.enter_context(tc.tile_pool(name="placed", bufs=1))
        offsets = lists.tile([P, S // LIST_ROWS], U16, name="offsets")

        def held(name, shape, dtype):
            return keep.tile(shape, dtype, name=name, align_bytes=64)

        at, free = {}, 0
        for row in ROWS:
            for name, size in row:
                at[name] = free
                free = free + size - LAP
            free = free + LAP
        for name, (host, shift) in INSIDE.items():
            at[name] = at[host] + shift

        def place(name, shape, dtype):
            return placed.tile(shape, dtype, name=name, align_bytes=64, offset=at[name])

        tab_sc = place("tab_sc", [P, T // 4], I32)
        v_sc_low = held("v_sc_low", [P, PASSES - 1, S // 4], I32)
        warm_in = held("warm_in", [P, 8], F32)
        warm_out = held("warm_out", [P, 8], F32)

        wb_sc_raw = place("wb_sc_raw", [P, PASSES, H // 4], I32)
        nc.gpsimd.memset(tab_sc[:], 0)
        nc.vector.memset(wb_sc_raw[:], 0)
        nc.vector.memset(warm_in[:], 0.0)
        nc.vector.memset(v_sc_low[:], 0)

        tab, wa_raw, g_tab = {}, {}, {}

        def load_tab(a):
            tab[a] = place(f"tab{a}", [P, T], I32)
            nc.sync.dma_start(tab[a][:], tab_words[a].rearrange("p n i -> p (n i)").bitcast(I32))

        def load_wa(a):
            rows = wa[a * P * PACK : (a + 1) * P * PACK, :]
            wa_raw[a] = place(f"wa_raw{a}", [P, PACK, H], F32)
            nc.sync.dma_start(wa_raw[a][:], rows.rearrange("(p j) c -> p j c", j=PACK))

        g_planes = gT.rearrange("(p t) n -> p t n", t=PACK)

        def load_g(t):
            g_tab[t] = place(f"g_tab{t}", [P, T], F32)
            nc.sync.dma_start(g_tab[t][:], g_planes[:, t, :])

        def load_tab_scales(q, queue):
            queue.dma_start(
                tab_sc[32 * q : 32 * q + 4 * PASSES, :], tab_scales[:, 4 * q : 4 * q + 4, :].bitcast(I32)
            )

        load_tab(0)
        nc.sync.dma_start(offsets[:], offs)
        for q in range(QUADS):
            load_tab_scales(q, (nc.sync, nc.scalar)[q // 2])
        load_tab(1)
        wb_raw = held("wb_raw", [P, PASSES, H // 2], I32)
        nc.sync.dma_start(wb_raw[:], wb_words.rearrange("a p c -> p a c").bitcast(I32))
        for q in range(QUADS):
            nc.sync.dma_start(
                wb_sc_raw[32 * q : 32 * q + 4, :, :],
                wb_scales[:, 4 * q : 4 * q + 4, :].rearrange("a r c -> r a c").bitcast(I32),
            )
        load_tab(2)
        load_wa(0)

        gain4 = held("gain4", [P, PACK], F32)
        nc.gpsimd.dma_start(gain4[:], gain.rearrange("(p t) -> p t", t=PACK))

        nc.scalar.activation(warm_out[:], warm_in[:], ACT.Sigmoid)

        wb_codes = held("wb_codes", [P, PASSES * H // 2], I32)
        nc.scalar.copy(
            wb_codes[:].bitcast(U16).rearrange("p (t c i) -> p c t i", t=PACK, i=8),
            wb_raw[:].bitcast(U16).rearrange("p a (c i t) -> p (a c) t i", t=PACK, i=8),
        )

        v_codes = {}

        def gather_words(a, whole):
            nc.vector.tensor_copy(whole[:], tab[a][:].bitcast(U32).indirect(offsets[:]))
            for h in range(HALVES):
                v_codes[a, h] = whole[:, h * HALF : (h + 1) * HALF]

        def entries(j0, width):
            return offsets[:, j0 // LIST_ROWS : (j0 + width) // LIST_ROWS]

        wb_sc = [held(f"wb_sc{a}", [P, H], U8) for a in range(PASSES)]
        for a in range(PASSES):
            nc.gpsimd.tensor_copy(
                wb_sc[a][:].rearrange("p (t m) -> p t m", t=PACK),
                wb_sc_raw[:, a, :].bitcast(U8).rearrange("p (m t) -> p t m", t=PACK),
            )
        def gather_half(a, h, tile):
            nc.vector.tensor_copy(tile[:], tab[a][:].bitcast(U32).indirect(entries(h * HALF, HALF)))
            v_codes[a, h] = tile[:]

        gather_half(0, 0, held("v_codes0_0", [P, HALF], U32))
        v_sc = held("v_sc", [P, S], U8)
        nc.vector.tensor_copy(v_sc[:], tab_sc[:].bitcast(U8).indirect(offsets[:]))
        for a in range(1, PASSES):
            nc.sync.dma_start(
                v_sc_low[0:SHIFT_ROWS, a - 1, :], v_sc[4 * a : 4 * a + SHIFT_ROWS, :].bitcast(I32)
            )
        load_wa(1)
        gather_half(0, 1, place("v_codes0_1", [P, HALF], U32))
        gather_words(1, held("v_codes1", [P, S], U32))
        load_wa(2)
        for h in range(HALVES):
            gather_half(2, h, (held, place)[h](f"v_codes2_{h}", [P, HALF], U32))
        load_g(0)

        wa_codes = [held(f"wa_codes{a}", [P, H], U32) for a in range(PASSES)]
        wa_sc = [held(f"wa_sc{a}", [P, H], U8) for a in range(PASSES)]

        def round_pair(copy):
            def run(grouped, raw, t0):
                copy(
                    grouped[:].rearrange("p (t m j) -> p m j t", t=PACK, j=PACK)[:, :, :, t0 : t0 + 2],
                    raw[:].rearrange("p j (m t) -> p m j t", t=PACK)[:, :, :, t0 : t0 + 2],
                )

            return run

        def round_pair_gpsimd(grouped, raw, t0):
            nc.gpsimd.tensor_copy(
                grouped[:].rearrange("p (t m j) -> p t m j", t=PACK, j=PACK)[:, t0 : t0 + 2, :, :],
                raw[:].rearrange("p j (m t) -> p t m j", t=PACK)[:, t0 : t0 + 2, :, :],
            )

        on_scalar, on_vector = round_pair(nc.scalar.copy), round_pair(nc.vector.tensor_copy)

        def quantize_wa(a, rounders):
            grouped = place(f"grouped{a}", [P, H * PACK], BF16)
            for t0, rounder in zip((0, 2), rounders):
                rounder(grouped, wa_raw[a], t0)
            parts = 2 if a == PASSES - 1 else 1
            for c0 in range(0, H, H // parts):
                cols = slice(c0, c0 + H // parts)
                nc.vector.quantize_mx(
                    out=wa_codes[a][:, cols].bitcast(FP8X4), scales=wa_sc[a][:, cols],
                    in_=grouped[:, PACK * cols.start : PACK * cols.stop],
                )

        quantize_wa(0, (on_scalar, round_pair_gpsimd))
        load_g(1)
        quantize_wa(1, (on_vector, on_vector))
        load_g(2)
        load_g(3)
        quantize_wa(2, (on_vector, on_vector))
        wo_codes = place("wo_codes", [P, N], I32)
        nc.sync.dma_start(wo_codes[:], wo_words[0].rearrange("p c i -> p (c i)").bitcast(I32))
        wo_sc = place("wo_sc", [P, N // 4], I32)
        nc.gpsimd.memset(wo_sc[:], 0)
        for q in range(QUADS):
            nc.sync.dma_start(
                wo_sc[32 * q : 32 * q + 4, :], wo_scales[0, 4 * q : 4 * q + 4, :].bitcast(I32)
            )

        banks, gate, content = {}, {}, {}

        def gate_pass(h, a, planes):
            cols = slice(h * HALF, (h + 1) * HALF)
            low = v_sc[:, cols] if a == 0 else v_sc_low[:, a - 1, :].bitcast(U8)[:, cols]
            for t in planes:
                m0 = P * (PASSES * t + a)
                nc.tensor.matmul_mx(
                    out=banks["gate", h][t][:],
                    lhsT=wb_codes[:].bitcast(U8)[:, 2 * m0 : 2 * (m0 + P)].bitcast(FP4X4),
                    lhsT_scale=wb_sc[a][:, P * t : P * (t + 1)],
                    rhs=v_codes[a, h].bitcast(FP8X4),
                    rhs_scale=low,
                    start=(a == 0),
                    stop=(a == PASSES - 1),
                )

        def content_pass(h, a, planes):
            cols = slice(h * HALF, (h + 1) * HALF)
            for t in planes:
                nc.tensor.matmul_mx(
                    out=banks["content", h][t][:],
                    lhsT=wa_codes[a][:, P * t : P * (t + 1)].bitcast(FP8X4),
                    lhsT_scale=wa_sc[a][:, P * t : P * (t + 1)],
                    rhs=v_codes[a, h].bitcast(FP8X4),
                    rhs_scale=v_sc[4 * a :, cols],
                    start=(a == 0),
                    stop=(a == PASSES - 1),
                )

        def take_banks(kind, h):
            banks[kind, h] = [psum.tile([P, HALF], F32, name="bank") for t in range(PACK)]

        def activate(kind, h, func, into):
            into[h] = (place if (kind, h) == ("gate", 0) else held)(f"{kind}{h}", [P, PACK, HALF], F32)
            for t in range(PACK):
                nc.scalar.activation(into[h][:, t, :], banks[kind, h][t][:], func)

        for h in range(HALVES):
            take_banks("gate", h)
        for h in range(HALVES):
            gate_pass(h, 0, range(PACK))
            for t in range(PACK):
                for a in range(1, PASSES):
                    gate_pass(h, a, (t,))
        for h in range(HALVES):
            activate("gate", h, ACT.Sigmoid, gate)
        GROUP = HALF // 2
        gained = held("gained", [P, PACK, HALF], F32)
        gained_third = place("gained_late", [P, PACK, GROUP], F32)
        for t in range(PACK):
            nc.gpsimd.tensor_scalar(
                gained_third[:, t, :], gate[1][:, t, :GROUP], gain4[:, t : t + 1], 0.0, ALU.mult, ALU.add
            )
        take_banks("content", 0)
        for a in range(PASSES):
            content_pass(0, a, range(PACK))
        content[0] = place("content0", [P, PACK, HALF], F32)

        def gain_gate(t):
            nc.scalar.activation(gained[:, t, :], gate[0][:, t, :], ACT.Copy, scale=gain4[:, t : t + 1])

        for t in range(PACK - 1):
            gain_gate(t)
        for t in range(PACK):
            if t == 2:
                gain_gate(PACK - 1)
            nc.scalar.activation(content[0][:, t, :], banks["content", 0][t][:], ACT.Tanh)
        take_banks("content", 1)
        for t in range(PACK):
            for a in range(PASSES):
                content_pass(1, a, (t,))
        activate("content", 1, ACT.Tanh, content)
        first = held("gated0", [P, PACK, HALF], F32)
        for t0 in (0, 2):
            nc.gpsimd.tensor_tensor(
                first[:, t0 : t0 + 2, :], content[0][:, t0 : t0 + 2, :], gained[:, t0 : t0 + 2, :], ALU.mult
            )
        third = held("gated512", [P, PACK, GROUP], F32)
        nc.gpsimd.tensor_tensor(third[:], content[1][:, :, :GROUP], gained_third[:], ALU.mult)

        picked, state = {}, {}
        for t in range(PACK - 1):
            whole = held(f"picked{t}", [P, S], F32)
            nc.vector.tensor_copy(whole[:], g_tab[t][:].indirect(offsets[:]))
            for h in range(HALVES):
                picked[t, h] = whole[:, h * HALF : (h + 1) * HALF]
        for h in range(HALVES):
            part = held(f"picked3_{h}", [P, HALF], F32)
            nc.vector.tensor_copy(part[:], g_tab[3][:].indirect(entries(h * HALF, HALF)))
            picked[3, h] = part[:]
        scaled = {}

        def scale_state(g0, width, planes):
            h, c0 = divmod(g0, HALF)
            if g0 not in scaled:
                scaled[g0] = place(f"state{g0}", [P, PACK, width], F32)
                for c in range(0, width, GROUP):
                    state[g0 + c] = scaled[g0][:, :, c : c + GROUP]
            for t in planes:
                nc.scalar.activation(
                    scaled[g0][:, t, :], picked[t, h][:, c0 : c0 + width], ACT.Copy, scale=gain4[:, t : t + 1]
                )

        scale_state(0, GROUP, range(PACK - 1))
        scale_state(HALF, HALF, range(PACK - 1))
        scale_state(0, GROUP, (PACK - 1,))
        scale_state(GROUP, GROUP, range(PACK))
        scale_state(HALF, HALF, (PACK - 1,))

        out_rows = out.rearrange("(c p) j -> p c j", p=P)
        staged, group_banks = {}, {}

        def multiply(bank, c0, codes, scales):
            for u in range(bank.shape[1]):
                n_cols = slice(P * (c0 + u), P * (c0 + u + 1))
                nc.tensor.matmul_mx(
                    out=bank[:, u, :],
                    lhsT=wo_codes[:, n_cols].bitcast(FP8X4),
                    lhsT_scale=wo_sc[:].bitcast(U8)[:, n_cols],
                    rhs=codes[:].bitcast(FP8X4),
                    rhs_scale=scales[:],
                    start=True,
                    stop=True,
                )

        def store(g0, c0, c1, cols):
            nc.sync.dma_start(out_rows[:, c0:c1, g0 + cols.start : g0 + cols.stop], staged[g0][:, c0:c1, cols])

        def project(h_grouped, j0):
            g0 = j0 - j0 % GROUP
            cols = slice(j0 - g0, j0 - g0 + PIECE)
            h_codes = ring2.tile([P, PIECE], U32, name="h_codes", align_bytes=64)
            h_sc = ring2.tile([P, PIECE], U8, name="h_sc", align_bytes=64)
            nc.vector.quantize_mx(out=h_codes[:].bitcast(FP8X4), scales=h_sc[:], in_=h_grouped[:])
            if j0 == g0:
                staged[g0] = place(f"staged{g0}", [P, CHUNKS, GROUP], F32)
            if g0 == 0:
                for c0 in range(0, CHUNKS, CHUNKS // 2):
                    c1 = c0 + CHUNKS // 2
                    bank = psum.tile([P, CHUNKS // 2, PIECE], F32, name="bank")
                    multiply(bank[:], c0, h_codes, h_sc)
                    nc.scalar.copy(staged[g0][:, c0:c1, cols], bank[:])
                    if j0 == 0:
                        store(g0, c0, c1, cols)
                if j0 > 0:
                    store(g0, 0, CHUNKS, cols)
                return
            per_bank = HALF // GROUP
            unsent = per_bank if g0 == S - GROUP else 0
            if unsent:
                bank = psum.tile([P, per_bank, PIECE], F32, name="bank")
                multiply(bank[:], 0, h_codes, h_sc)
                nc.scalar.copy(staged[g0][:, :per_bank, cols], bank[:])
                store(g0, 0, per_bank, cols)
            late = range(unsent, CHUNKS, per_bank)
            if j0 == g0:
                group_banks[g0] = [psum.tile([P, per_bank, GROUP], F32, name="bank") for c0 in late]
            for c0, bank in zip(late, group_banks[g0]):
                multiply(bank[:, :, cols], c0, h_codes, h_sc)
                if j0 > g0:
                    c1 = c0 + per_bank
                    on_vector = g0 == S - GROUP and c0 == per_bank
                    (nc.vector.tensor_copy if on_vector else nc.scalar.copy)(staged[g0][:, c0:c1, :], bank[:])
                    if c1 in STORE_ENDS[g0]:
                        store(g0, unsent, c1, slice(0, GROUP))
                        unsent = c1

        def product_on_vector(j0):
            cols = slice(j0 - HALF, j0 - HALF + PIECE)
            product = place(f"gated{j0}", [P, PACK, PIECE], F32)
            for t in range(PACK):
                nc.vector.scalar_tensor_tensor(
                    product[:, t, :], content[1][:, t, cols], gain4[:, t : t + 1],
                    gate[1][:, t, cols], ALU.mult, ALU.mult,
                )
            return product[:]

        gated = {j0: first[:, :, j0 : j0 + PIECE] for j0 in range(0, HALF, PIECE)}
        for c0 in range(0, GROUP, PIECE):
            gated[HALF + c0] = third[:, :, c0 : c0 + PIECE]
        for j0 in range(0, S, PIECE):
            g0 = j0 - j0 % GROUP
            if j0 == S - GROUP:
                gated[j0] = product_on_vector(j0)
            h_grouped = (place if j0 == HALF - PIECE else held)(f"h_grouped{j0}", [P, PIECE * PACK], BF16)
            nc.vector.tensor_tensor(
                h_grouped[:].rearrange("p (c i t) -> p c t i", i=2, t=PACK),
                gated[j0].rearrange("p t (c i) -> p c t i", i=2),
                state[g0][:, :, j0 - g0 : j0 - g0 + PIECE].rearrange("p t (c i) -> p c t i", i=2),
                ALU.add,
            )
            if j0 == S - GROUP:
                gated[j0 + PIECE] = product_on_vector(j0 + PIECE)
            project(h_grouped, j0)
